import numpy as np
import ml_dtypes


def mxq(x, axis, fmt="e4m3"):
    dtype, down = {"e4m3": (ml_dtypes.float8_e4m3fn, 7), "e5m2": (ml_dtypes.float8_e5m2, 14)}[fmt]
    v = np.moveaxis(np.asarray(x, np.float32).astype(ml_dtypes.bfloat16).astype(np.float64), axis, -1)
    blocks = v.reshape(v.shape[:-1] + (-1, 32))
    amax = np.abs(blocks).max(-1, keepdims=True)
    byte = np.maximum(np.where(amax > 0, np.frexp(amax)[1] - 1 + 127, 0) - down, 1)
    scale = np.exp2(byte - 127.0)
    codes = (blocks / scale).astype(np.float32).astype(dtype).astype(np.float64)
    return np.moveaxis((codes * scale).reshape(v.shape), -1, axis)


WIDE = False


def mx_kscale(k):
    if not WIDE:
        return np.ones(k)
    levels = np.array([10, -10, 5, -5, 0])
    if k % 512:
        return np.exp2(np.random.permutation(np.resize(levels, k // 32))).repeat(32)
    a = np.empty((k // 512, 16))
    for p in range(k // 512):
        a[p, :8] = np.random.permutation(np.resize(levels, 8))
        for g in range(8):
            far = levels[np.abs(levels - a[p, g]) >= 10]
            a[p, g + 8] = far[np.random.randint(len(far))]
    return np.exp2(a.ravel()).repeat(32)


def f64(x):
    return np.asarray(x).astype(np.float64)


def striped8(idx):
    return np.concatenate([x.reshape(-1, 16).T for x in idx]).astype(np.uint16)


def runs(offs, k):
    lists = np.stack([offs[16 * r : 16 * r + 16].T.reshape(-1) for r in range(8)]).astype(np.int64)
    return lists[np.arange(k) % 512 // 64]


def pack_weight(w):
    k, n = w.shape
    w = f64(np.asarray(w, np.float32).astype(ml_dtypes.bfloat16)).reshape(k // 32, 32, n)
    amax = np.abs(w).max(1)
    byte = np.clip(np.where(amax > 0, np.frexp(amax)[1] - 1 + 127 - 7, 1), 1, 254)
    scaled = (w * np.exp2(127.0 - byte)[:, None, :]).reshape(k, n).astype(np.float32)
    words = np.ascontiguousarray(scaled.reshape(k // 512, 128, 4, n).transpose(0, 1, 3, 2)).astype(ml_dtypes.float8_e4m3fn).view(np.uint8)
    return words, np.ascontiguousarray(byte.astype(np.uint8).reshape(k // 512, 16, n))


def unpack_weight(words, scales):
    g, p, n, _ = words.shape
    vals = np.ascontiguousarray(words).view(ml_dtypes.float8_e4m3fn).astype(np.float64) * np.repeat(np.exp2(scales.astype(np.float64) - 127.0), 8, axis=1)[..., None]
    return vals.transpose(0, 1, 3, 2).reshape(g * 512, n)


def gelu(v):
    return 0.5 * v * (1.0 + np.tanh(np.sqrt(2.0 / np.pi) * (v + 0.044715 * v**3)))


K, T, S, H, N, V = 1024, 2048, 1024, 512, 256, 512


def setup_inputs():
    n = np.random.standard_normal
    s = mx_kscale(K)[:, None]
    u = mx_kscale(H)
    packed_xT = pack_weight(n((K, T)) * s)
    return {
        "x_words": packed_xT[0],
        "x_scales": packed_xT[1],
        "w1": (n((K, H)) / np.sqrt(K) / s * u).astype(np.float32),
        "w2": (n((H, N)) / np.sqrt(H) / u[:, None]).astype(np.float32),
        "offs": striped8(np.stack([np.random.permutation(T)[:S] for _ in range(8)])),
    }


def reference(x_words, x_scales, w1, w2, offs):
    xq = unpack_weight(x_words, x_scales)[np.arange(K)[:, None], runs(offs, K)]
    y = mxq(f64(w1), 0, "e4m3").T @ xq
    z = np.maximum(y[:, :V], y[:, V:2 * V])
    za = gelu(z)
    return mxq(f64(w2), 0, "e4m3").T @ mxq(za, 0, "e4m3")

@@ -1,0 +1,199 @@
+from contextlib import ExitStack
+
+import concourse.mybir as mybir
+
+K, T, S, H, N, V = 1024, 2048, 1024, 512, 256, 512
+FLOPS = 2 * K * H * S + 2 * H * N * V
+
+F32 = mybir.dt.float32
+BF16 = mybir.dt.bfloat16
+I32 = mybir.dt.int32
+U32 = mybir.dt.uint32
+U16 = mybir.dt.uint16
+U8 = mybir.dt.uint8
+FP8X4 = mybir.dt.float8_e4m3fn_x4
+GELU = mybir.ActivationFunctionType.Gelu_apprx_tanh
+MAX = mybir.AluOpType.max
+
+P = 128
+PACK = 4
+PASSES = K // (P * PACK)
+CHUNK = 256
+CHUNKS = V // CHUNK
+LIST_ROWS = 16
+HALF = H // 2
+HM = HALF // PACK
+
+
+def tile_picked_phpool_gelu_p_kernel(tc, x_words, x_scales, w1, w2, offs, out):
+    nc = tc.nc
+    with ExitStack() as ctx:
+        keep = ctx.enter_context(tc.tile_pool(name="keep", bufs=1))
+        psum = ctx.enter_context(tc.psum_pool(name="psum", bufs=1))
+
+        offsets = keep.tile([P, S // LIST_ROWS], U16, name="offsets")
+        nc.sync.dma_start(offsets[:], offs)
+
+        scale_table = keep.tile([P, T], U8, name="scale_table", tag="scale_table_then_words", align_bytes=64)
+        nc.vector.memset(scale_table[:].bitcast(I32), 0)
+        zero = keep.tile([P, 1], F32, name="zero")
+        nc.vector.memset(zero[:], 0.0)
+        warm = keep.tile([P, 1], F32, name="warm")
+        nc.scalar.activation(warm[:], zero[:], GELU)
+        for z in range(PASSES):
+            for e in range(2):
+                nc.scalar.dma_start(
+                    scale_table[4 * z + e : P : LIST_ROWS, :].bitcast(I32),
+                    x_scales[z, e : 16 : 2, :].bitcast(I32),
+                )
+
+        w1_rows = [w1[512 * z : 512 * (z + 1), :].rearrange("(p j) c -> p j c", j=PACK) for z in range(PASSES)]
+        w1a_raw = keep.tile([P, PACK, H], F32, name="w1a_raw")
+        nc.sync.dma_start(w1a_raw[:], w1_rows[0])
+        word_table = []
+        for z in range(PASSES):
+            table = keep.tile([P, T], I32, name="word_table%d" % z)
+            nc.sync.dma_start(table[:], x_words[z].rearrange("p n t -> p (n t)").bitcast(I32))
+            word_table.append(table)
+        w1b_raw = []
+        for h in range(2):
+            raw = keep.tile([P, PACK, HALF], F32, name="w1b_raw%d" % h)
+            nc.sync.dma_start(raw[:], w1_rows[1][:, :, HALF * h : HALF * (h + 1)])
+            w1b_raw.append(raw)
+        w2_raw = keep.tile([P, PACK, N], F32, name="w2_raw")
+        nc.sync.dma_start(w2_raw[:], w2.rearrange("(p j) n -> p j n", j=PACK))
+
+        def list_slice(c, r):
+            first = (r * V + c * CHUNK) // LIST_ROWS
+            return offsets[:, first : first + CHUNK // LIST_ROWS]
+
+        picked_scales = keep.tile([P, S], U8, name="picked_scales", align_bytes=64)
+        for c in range(CHUNKS):
+            for r in range(2):
+                at = (2 * c + r) * CHUNK
+                nc.vector.tensor_copy(picked_scales[:, at : at + CHUNK], scale_table[:].indirect(list_slice(c, r)))
+        planes = keep.tile([P, S], U8, name="planes", align_bytes=64)
+        nc.vector.tensor_copy(planes[:].bitcast(I32), picked_scales[:].bitcast(I32))
+        for z in range(PASSES):
+            for e in range(2):
+                nc.scalar.dma_start(
+                    planes[4 * z + 2 + e : P : 32, :].bitcast(I32),
+                    picked_scales[16 + 4 * z + e : P : 32, :].bitcast(I32),
+                )
+
+        w1_codes = [keep.tile([P, H], U32, name="w1_codes%d" % z, align_bytes=64) for z in range(PASSES)]
+        w1_scales = [keep.tile([P, H], U8, name="w1_scales%d" % z, align_bytes=64) for z in range(PASSES)]
+
+        def deal(copy, grouped, raw_half, m0, m1):
+            copy(
+                grouped[:].rearrange("p (t m j) -> p m j t", t=PACK, j=PACK)[:, m0:m1],
+                raw_half.rearrange("p j (m t) -> p m j t", t=PACK)[:, m0:m1],
+            )
+
+        def quantize_half(z, h, grouped):
+            for t in range(PACK):
+                cols = slice(P * t + HM * h, P * t + HM * (h + 1))
+                nc.vector.quantize_mx(
+                    out=w1_codes[z][:, cols].bitcast(FP8X4),
+                    scales=w1_scales[z][:, cols],
+                    in_=grouped[:, HALF * t : HALF * (t + 1)],
+                )
+
+        def gather_words(z, c, tag):
+            words = keep.tile([P, 2 * CHUNK], U32, name="picked_words%d%d" % (z, c), tag=tag, align_bytes=64)
+            for r in range(2):
+                nc.vector.tensor_copy(
+                    words[:, r * CHUNK : (r + 1) * CHUNK], word_table[z][:].bitcast(U32).indirect(list_slice(c, r))
+                )
+            return words
+
+        grouped = [
+            [keep.tile([P, PACK * HALF], BF16, name="w1_grouped%d%d" % (z, h), align_bytes=64) for h in range(2)]
+            for z in range(PASSES)
+        ]
+        deal(nc.scalar.copy, grouped[0][0], w1a_raw[:, :, 0:HALF], 0, HM)
+        deal(nc.vector.tensor_copy, grouped[0][1], w1a_raw[:, :, HALF:H], 0, HM)
+        quantize_half(0, 0, grouped[0][0])
+        quantize_half(0, 1, grouped[0][1])
+
+        banks = [[psum.tile([P, 2 * CHUNK], F32, name="y%d%d" % (c, t), tag="bank%d" % (4 * c + t)) for t in range(PACK)] for c in range(CHUNKS)]
+
+        def first_product(z, c, words):
+            for t in range(PACK):
+                nc.tensor.matmul_mx(
+                    out=banks[c][t][:],
+                    lhsT=w1_codes[z][:, P * t : P * (t + 1)].bitcast(FP8X4),
+                    lhsT_scale=w1_scales[z][:, P * t : P * (t + 1)],
+                    rhs=words[:].bitcast(FP8X4),
+                    rhs_scale=planes[4 * z : P, 2 * CHUNK * c : 2 * CHUNK * (c + 1)],
+                    start=(z == 0),
+                    stop=(z == PASSES - 1),
+                )
+
+        for c in range(CHUNKS):
+            words = gather_words(0, c, "scale_table_then_words" if c == 0 else "words01")
+            first_product(0, c, words)
+        last_words = [gather_words(1, c, "words1%d" % c) for c in range(CHUNKS)]
+
+        deal(nc.scalar.copy, grouped[1][0], w1b_raw[0][:], 0, HM)
+        deal(nc.vector.tensor_copy, grouped[1][1], w1b_raw[1][:], 0, 44)
+        deal(nc.scalar.copy, grouped[1][1], w1b_raw[1][:], 44, HM)
+        quantize_half(1, 0, grouped[1][0])
+        quantize_half(1, 1, grouped[1][1])
+
+        larger = []
+        for c in range(CHUNKS):
+            first_product(1, c, last_words[c])
+        w2_grouped = keep.tile([P, PACK * N], BF16, name="w2_grouped", align_bytes=64)
+        w2_codes = keep.tile([P, N], U32, name="w2_codes", align_bytes=64)
+        w2_scales = keep.tile([P, N], U8, name="w2_scales", align_bytes=64)
+        nc.vector.tensor_copy(
+            w2_grouped[:].rearrange("p (c i j) -> p c j i", i=4, j=PACK),
+            w2_raw[:].rearrange("p j (c i) -> p c j i", i=4),
+        )
+        for c in range(CHUNKS):
+            big = keep.tile([P, PACK, CHUNK], F32, name="larger%d" % c)
+            larger.append(big)
+            for t in range(PACK):
+                if c == CHUNKS - 1 and t == PACK - 1:
+                    nc.vector.tensor_reduce(
+                        big[:, t, :], banks[c][t][:].rearrange("p (r v) -> p v r", r=2), mybir.AxisListType.X, MAX
+                    )
+                else:
+                    first = keep.tile([P, CHUNK], F32, name="first_read%d%d" % (c, t))
+                    nc.scalar.copy(first[:], banks[c][t][:, 0:CHUNK])
+                    nc.vector.tensor_tensor(big[:, t, :], first[:], banks[c][t][:, CHUNK : 2 * CHUNK], MAX)
+            if c == 0:
+                nc.vector.quantize_mx(out=w2_codes[:].bitcast(FP8X4), scales=w2_scales[:], in_=w2_grouped[:])
+
+        out_rows = out.rearrange("(h p) v -> p h v", p=P)
+        pieces = [(0, 0, 256, (0, 1)), (1, 0, 128, (2, 3)), (1, 128, 128, (4, 5))]
+        for c, v0, n, tags in pieces:
+            name = "%d_%d" % (c, v0)
+            z_grouped = keep.tile([P, PACK * n], BF16, name="z_grouped" + name, align_bytes=64)
+            nc.scalar.activation(
+                z_grouped[:].rearrange("p (c i t) -> p c t i", i=4, t=PACK),
+                larger[c][:, :, v0 : v0 + n].rearrange("p t (c i) -> p c t i", i=4),
+                GELU,
+            )
+            z_codes = keep.tile([P, n], U32, name="z_codes" + name, align_bytes=64)
+            z_scales = keep.tile([P, n], U8, name="z_scales" + name, align_bytes=64)
+            nc.vector.quantize_mx(out=z_codes[:].bitcast(FP8X4), scales=z_scales[:], in_=z_grouped[:])
+            result = keep.tile([P, 2, n], F32, name="result" + name)
+            for h in range(2):
+                acc = psum.tile([P, n], F32, name="acc%s_%d" % (name, h), tag="bank%d" % tags[h])
+                nc.tensor.matmul_mx(
+                    out=acc[:],
+                    lhsT=w2_codes[:, P * h : P * (h + 1)].bitcast(FP8X4),
+                    lhsT_scale=w2_scales[:, P * h : P * (h + 1)],
+                    rhs=z_codes[:].bitcast(FP8X4),
+                    rhs_scale=z_scales[:],
+                    start=True,
+                    stop=True,
+                )
+                if h == 1 and v0 > 0:
+                    nc.scalar.copy(result[:, h, :], acc[:])
+                else:
+                    nc.vector.tensor_copy(result[:, h, :], acc[:])
+            first_v = c * CHUNK + v0
+            nc.sync.dma_start(out_rows[:, :, first_v : first_v + n], result[:])

@@ -31,30 +31,48 @@ def tile_picked_phpool_gelu_p_kernel(tc, x_words, x_scales, w1, w2, offs, out):
         keep = ctx.enter_context(tc.tile_pool(name="keep", bufs=1))
         psum = ctx.enter_context(tc.psum_pool(name="psum", bufs=1))
 
+        w1_rows = [w1[512 * z : 512 * (z + 1), :].rearrange("(p j) c -> p j c", j=PACK) for z in range(PASSES)]
+        x_rows = [x_words[z].rearrange("p n t -> p (n t)").bitcast(I32) for z in range(PASSES)]
+        word_table = [keep.tile([P, T], I32, name="word_table%d" % z) for z in range(PASSES)]
+        w1a_raw = [keep.tile([P, PACK, HALF], F32, name="w1a_raw%d" % h) for h in range(2)]
+        nc.sync.dma_start(w1a_raw[0][:], w1_rows[0][:, :, 0:HALF])
         offsets = keep.tile([P, S // LIST_ROWS], U16, name="offsets")
         nc.sync.dma_start(offsets[:], offs)
 
         scale_table = keep.tile([P, T], U8, name="scale_table", tag="scale_table_then_words", align_bytes=64)
         nc.vector.memset(scale_table[:].bitcast(I32), 0)
+        for z in range(PASSES):
+            for e in range(2):
+                (nc.sync if e == 0 else nc.scalar).dma_start(
+                    scale_table[4 * z + e : P : LIST_ROWS, :].bitcast(I32),
+                    x_scales[z, e : 16 : 2, :].bitcast(I32),
+                )
         zero = keep.tile([P, 1], F32, name="zero")
         nc.vector.memset(zero[:], 0.0)
         warm = keep.tile([P, 1], F32, name="warm")
         nc.scalar.activation(warm[:], zero[:], GELU)
+
+        nc.sync.dma_start(w1a_raw[1][:], w1_rows[0][:, :, HALF:H])
+        nc.sync.dma_start(word_table[0][:], x_rows[0])
+        nc.sync.dma_start(word_table[1][:], x_rows[1])
+
+        def list_slice(c, r):
+            first = (r * V + c * CHUNK) // LIST_ROWS
+            return offsets[:, first : first + CHUNK // LIST_ROWS]
+
+        picked_scales = keep.tile([P, S], U8, name="picked_scales", align_bytes=64)
+        nc.vector.tensor_copy(picked_scales[:], scale_table[:].indirect(offsets[:]))
+        planes = keep.tile([P, S], U8, name="planes", align_bytes=64)
+        nc.vector.tensor_copy(
+            planes[:].bitcast(I32).rearrange("p (c r w) -> p c r w", c=CHUNKS, r=2),
+            picked_scales[:].bitcast(I32).rearrange("p (r c w) -> p c r w", c=CHUNKS, r=2),
+        )
         for z in range(PASSES):
             for e in range(2):
-                nc.scalar.dma_start(
-                    scale_table[4 * z + e : P : LIST_ROWS, :].bitcast(I32),
-                    x_scales[z, e : 16 : 2, :].bitcast(I32),
+                nc.sync.dma_start(
+                    planes[4 * z + 2 + e : P : 32, :].bitcast(I32),
+                    planes[16 + 4 * z + e : P : 32, :].bitcast(I32),
                 )
-
-        w1_rows = [w1[512 * z : 512 * (z + 1), :].rearrange("(p j) c -> p j c", j=PACK) for z in range(PASSES)]
-        w1a_raw = keep.tile([P, PACK, H], F32, name="w1a_raw")
-        nc.sync.dma_start(w1a_raw[:], w1_rows[0])
-        word_table = []
-        for z in range(PASSES):
-            table = keep.tile([P, T], I32, name="word_table%d" % z)
-            nc.sync.dma_start(table[:], x_words[z].rearrange("p n t -> p (n t)").bitcast(I32))
-            word_table.append(table)
         w1b_raw = []
         for h in range(2):
             raw = keep.tile([P, PACK, HALF], F32, name="w1b_raw%d" % h)
@@ -63,41 +81,15 @@ def tile_picked_phpool_gelu_p_kernel(tc, x_words, x_scales, w1, w2, offs, out):
         w2_raw = keep.tile([P, PACK, N], F32, name="w2_raw")
         nc.sync.dma_start(w2_raw[:], w2.rearrange("(p j) n -> p j n", j=PACK))
 
-        def list_slice(c, r):
-            first = (r * V + c * CHUNK) // LIST_ROWS
-            return offsets[:, first : first + CHUNK // LIST_ROWS]
-
-        picked_scales = keep.tile([P, S], U8, name="picked_scales", align_bytes=64)
-        for c in range(CHUNKS):
-            for r in range(2):
-                at = (2 * c + r) * CHUNK
-                nc.vector.tensor_copy(picked_scales[:, at : at + CHUNK], scale_table[:].indirect(list_slice(c, r)))
-        planes = keep.tile([P, S], U8, name="planes", align_bytes=64)
-        nc.vector.tensor_copy(planes[:].bitcast(I32), picked_scales[:].bitcast(I32))
-        for z in range(PASSES):
-            for e in range(2):
-                nc.scalar.dma_start(
-                    planes[4 * z + 2 + e : P : 32, :].bitcast(I32),
-                    picked_scales[16 + 4 * z + e : P : 32, :].bitcast(I32),
-                )
 
         w1_codes = [keep.tile([P, H], U32, name="w1_codes%d" % z, align_bytes=64) for z in range(PASSES)]
         w1_scales = [keep.tile([P, H], U8, name="w1_scales%d" % z, align_bytes=64) for z in range(PASSES)]
 
-        def deal(copy, grouped, raw_half, m0, m1):
+        def deal(copy, grouped, m_first, raw, m0, m1):
             copy(
-                grouped[:].rearrange("p (t m j) -> p m j t", t=PACK, j=PACK)[:, m0:m1],
-                raw_half.rearrange("p j (m t) -> p m j t", t=PACK)[:, m0:m1],
+                grouped[:].rearrange("p (t m j) -> p m j t", t=PACK, j=PACK)[:, m_first + m0 : m_first + m1],
+                raw.rearrange("p j (m t) -> p m j t", t=PACK)[:, m0:m1],
             )
-
-        def quantize_half(z, h, grouped):
-            for t in range(PACK):
-                cols = slice(P * t + HM * h, P * t + HM * (h + 1))
-                nc.vector.quantize_mx(
-                    out=w1_codes[z][:, cols].bitcast(FP8X4),
-                    scales=w1_scales[z][:, cols],
-                    in_=grouped[:, HALF * t : HALF * (t + 1)],
-                )
 
         def gather_words(z, c, tag):
             words = keep.tile([P, 2 * CHUNK], U32, name="picked_words%d%d" % (z, c), tag=tag, align_bytes=64)
@@ -107,14 +99,11 @@ def tile_picked_phpool_gelu_p_kernel(tc, x_words, x_scales, w1, w2, offs, out):
                 )
             return words
 
-        grouped = [
-            [keep.tile([P, PACK * HALF], BF16, name="w1_grouped%d%d" % (z, h), align_bytes=64) for h in range(2)]
-            for z in range(PASSES)
+        w1_grouped = [
+            keep.tile([P, PACK * H], BF16, name="w1_grouped%d" % z, tag="grouped%d" % z, align_bytes=64) for z in range(PASSES)
         ]
-        deal(nc.scalar.copy, grouped[0][0], w1a_raw[:, :, 0:HALF], 0, HM)
-        deal(nc.vector.tensor_copy, grouped[0][1], w1a_raw[:, :, HALF:H], 0, HM)
-        quantize_half(0, 0, grouped[0][0])
-        quantize_half(0, 1, grouped[0][1])
+        for h in range(2):
+            deal(nc.scalar.copy, w1_grouped[0], HM * h, w1a_raw[h][:], 0, HM)
 
         banks = [[psum.tile([P, 2 * CHUNK], F32, name="y%d%d" % (c, t), tag="bank%d" % (4 * c + t)) for t in range(PACK)] for c in range(CHUNKS)]
 
@@ -130,60 +119,69 @@ def tile_picked_phpool_gelu_p_kernel(tc, x_words, x_scales, w1, w2, offs, out):
                     stop=(z == PASSES - 1),
                 )
 
+        nc.vector.quantize_mx(out=w1_codes[0][:].bitcast(FP8X4), scales=w1_scales[0][:], in_=w1_grouped[0][:])
+        first_words = [gather_words(0, c, "scale_table_then_words" if c == 0 else "words01") for c in range(CHUNKS)]
         for c in range(CHUNKS):
-            words = gather_words(0, c, "scale_table_then_words" if c == 0 else "words01")
-            first_product(0, c, words)
+            first_product(0, c, first_words[c])
         last_words = [gather_words(1, c, "words1%d" % c) for c in range(CHUNKS)]
 
-        deal(nc.scalar.copy, grouped[1][0], w1b_raw[0][:], 0, HM)
-        deal(nc.vector.tensor_copy, grouped[1][1], w1b_raw[1][:], 0, 44)
-        deal(nc.scalar.copy, grouped[1][1], w1b_raw[1][:], 44, HM)
-        quantize_half(1, 0, grouped[1][0])
-        quantize_half(1, 1, grouped[1][1])
-
-        larger = []
+        deal(nc.scalar.copy, w1_grouped[1], 0, w1b_raw[0][:], 0, HM)
+        deal(nc.scalar.copy, w1_grouped[1], HM, w1b_raw[1][:], 0, HM)
+        for t in range(PACK):
+            nc.vector.quantize_mx(
+                out=w1_codes[1][:, P * t : P * (t + 1)].bitcast(FP8X4),
+                scales=w1_scales[1][:, P * t : P * (t + 1)],
+                in_=w1_grouped[1][:, H * t : H * (t + 1)],
+            )
         for c in range(CHUNKS):
             first_product(1, c, last_words[c])
+
         w2_grouped = keep.tile([P, PACK * N], BF16, name="w2_grouped", align_bytes=64)
         w2_codes = keep.tile([P, N], U32, name="w2_codes", align_bytes=64)
         w2_scales = keep.tile([P, N], U8, name="w2_scales", align_bytes=64)
-        nc.vector.tensor_copy(
-            w2_grouped[:].rearrange("p (c i j) -> p c j i", i=4, j=PACK),
-            w2_raw[:].rearrange("p j (c i) -> p c j i", i=4),
+        nc.scalar.copy(
+            w2_grouped[:].rearrange("p (c i j) -> p c j i", i=4, j=PACK), w2_raw[:].rearrange("p j (c i) -> p c j i", i=4)
         )
-        for c in range(CHUNKS):
-            big = keep.tile([P, PACK, CHUNK], F32, name="larger%d" % c)
-            larger.append(big)
-            for t in range(PACK):
-                if c == CHUNKS - 1 and t == PACK - 1:
-                    nc.vector.tensor_reduce(
-                        big[:, t, :], banks[c][t][:].rearrange("p (r v) -> p v r", r=2), mybir.AxisListType.X, MAX
-                    )
-                else:
-                    first = keep.tile([P, CHUNK], F32, name="first_read%d%d" % (c, t))
-                    nc.scalar.copy(first[:], banks[c][t][:, 0:CHUNK])
-                    nc.vector.tensor_tensor(big[:, t, :], first[:], banks[c][t][:, CHUNK : 2 * CHUNK], MAX)
-            if c == 0:
-                nc.vector.quantize_mx(out=w2_codes[:].bitcast(FP8X4), scales=w2_scales[:], in_=w2_grouped[:])
 
-        out_rows = out.rearrange("(h p) v -> p h v", p=P)
-        pieces = [(0, 0, 256, (0, 1)), (1, 0, 128, (2, 3)), (1, 128, 128, (4, 5))]
-        for c, v0, n, tags in pieces:
-            name = "%d_%d" % (c, v0)
-            z_grouped = keep.tile([P, PACK * n], BF16, name="z_grouped" + name, align_bytes=64)
+        largers = []
+        for c in range(CHUNKS):
+            larger = keep.tile([P, PACK, CHUNK], F32, name="larger%d" % c)
+            largers.append(larger)
+            for t in range(PACK):
+                reads = banks[c][t][:].rearrange("p (r v) -> p r v", r=2)
+                if (c, t) in ((0, 0), (CHUNKS - 1, PACK - 1)):
+                    nc.vector.tensor_reduce(larger[:, t, :], reads.rearrange("p r v -> p v r"), mybir.AxisListType.X, MAX)
+                else:
+                    first_read = keep.tile([P, CHUNK], F32, name="first_read%d%d" % (c, t))
+                    nc.scalar.copy(first_read[:], reads[:, 0, :])
+                    nc.vector.tensor_tensor(larger[:, t, :], first_read[:], reads[:, 1, :], MAX)
+                if (c, t) == (0, 0):
+                    nc.vector.quantize_mx(out=w2_codes[:].bitcast(FP8X4), scales=w2_scales[:], in_=w2_grouped[:])
+
+        pieces = [(0, 0, 256), (1, 0, 128), (1, 128, 128)]
+        z_grouped = []
+        for c, v0, n in pieces:
+            grouped = keep.tile([P, PACK * n], BF16, name="z_grouped%d_%d" % (c, v0), align_bytes=64)
             nc.scalar.activation(
-                z_grouped[:].rearrange("p (c i t) -> p c t i", i=4, t=PACK),
-                larger[c][:, :, v0 : v0 + n].rearrange("p t (c i) -> p c t i", i=4),
+                grouped[:].rearrange("p (c i t) -> p c t i", i=4, t=PACK),
+                largers[c][:, :, v0 : v0 + n].rearrange("p t (c i) -> p c t i", i=4),
                 GELU,
             )
-            z_codes = keep.tile([P, n], U32, name="z_codes" + name, align_bytes=64)
-            z_scales = keep.tile([P, n], U8, name="z_scales" + name, align_bytes=64)
-            nc.vector.quantize_mx(out=z_codes[:].bitcast(FP8X4), scales=z_scales[:], in_=z_grouped[:])
-            result = keep.tile([P, 2, n], F32, name="result" + name)
+            z_grouped.append(grouped)
+
+        out_rows = out.rearrange("(h p) v -> p h v", p=P)
+        for i, (c, v0, n) in enumerate(pieces):
+            z_codes = keep.tile([P, n], U32, name="z_codes%d" % i, align_bytes=64)
+            z_scales = keep.tile([P, n], U8, name="z_scales%d" % i, align_bytes=64)
+            nc.vector.quantize_mx(out=z_codes[:].bitcast(FP8X4), scales=z_scales[:], in_=z_grouped[i][:])
+            if i == 1:
+                both = psum.tile([P, 2, n], F32, name="acc%d" % i, tag="bank2")
+                accs = [both[:, h, :] for h in range(2)]
+            else:
+                accs = [psum.tile([P, n], F32, name="acc%d_%d" % (i, h), tag="bank%d" % (3 * i // 2 + h))[:] for h in range(2)]
             for h in range(2):
-                acc = psum.tile([P, n], F32, name="acc%s_%d" % (name, h), tag="bank%d" % tags[h])
                 nc.tensor.matmul_mx(
-                    out=acc[:],
+                    out=accs[h],
                     lhsT=w2_codes[:, P * h : P * (h + 1)].bitcast(FP8X4),
                     lhsT_scale=w2_scales[:, P * h : P * (h + 1)],
                     rhs=z_codes[:].bitcast(FP8X4),
@@ -191,9 +189,17 @@ def tile_picked_phpool_gelu_p_kernel(tc, x_words, x_scales, w1, w2, offs, out):
                     start=True,
                     stop=True,
                 )
-                if h == 1 and v0 > 0:
-                    nc.scalar.copy(result[:, h, :], acc[:])
+            cols = slice(c * CHUNK + v0, c * CHUNK + v0 + n)
+            if i == 0:
+                for h, copy in enumerate((nc.vector.tensor_copy, nc.scalar.copy)):
+                    half = keep.tile([P, n], F32, name="result0_%d" % h)
+                    copy(half[:], accs[h])
+                    nc.sync.dma_start(out_rows[:, h, cols], half[:])
+            else:
+                result = keep.tile([P, 2, n], F32, name="result%d" % i)
+                if i == 1:
+                    nc.vector.tensor_copy(result[:], both[:])
                 else:
-                    nc.vector.tensor_copy(result[:, h, :], acc[:])
-            first_v = c * CHUNK + v0
-            nc.sync.dma_start(out_rows[:, :, first_v : first_v + n], result[:])
+                    nc.vector.tensor_copy(result[:, 0, :], accs[0])
+                    nc.scalar.copy(result[:, 1, :], accs[1])
+                nc.sync.dma_start(out_rows[:, :, cols], result[:])

@@ -43,7 +43,7 @@ def tile_picked_phpool_gelu_p_kernel(tc, x_words, x_scales, w1, w2, offs, out):
         nc.vector.memset(scale_table[:].bitcast(I32), 0)
         for z in range(PASSES):
             for e in range(2):
-                (nc.sync if e == 0 else nc.scalar).dma_start(
+                nc.sync.dma_start(
                     scale_table[4 * z + e : P : LIST_ROWS, :].bitcast(I32),
                     x_scales[z, e : 16 : 2, :].bitcast(I32),
                 )
@@ -87,8 +87,8 @@ def tile_picked_phpool_gelu_p_kernel(tc, x_words, x_scales, w1, w2, offs, out):
 
         def deal(copy, grouped, m_first, raw, m0, m1):
             copy(
-                grouped[:].rearrange("p (t m j) -> p m j t", t=PACK, j=PACK)[:, m_first + m0 : m_first + m1],
-                raw.rearrange("p j (m t) -> p m j t", t=PACK)[:, m0:m1],
+                grouped[:].rearrange("p (t m j) -> p m t j", t=PACK, j=PACK)[:, m_first + m0 : m_first + m1],
+                raw.rearrange("p j (m t) -> p m t j", t=PACK)[:, m0:m1],
             )
 
         def gather_words(z, c, tag):
@@ -126,12 +126,13 @@ def tile_picked_phpool_gelu_p_kernel(tc, x_words, x_scales, w1, w2, offs, out):
         last_words = [gather_words(1, c, "words1%d" % c) for c in range(CHUNKS)]
 
         deal(nc.scalar.copy, w1_grouped[1], 0, w1b_raw[0][:], 0, HM)
-        deal(nc.scalar.copy, w1_grouped[1], HM, w1b_raw[1][:], 0, HM)
-        for t in range(PACK):
+        deal(nc.scalar.copy, w1_grouped[1], HM, w1b_raw[1][:], 0, 44)
+        deal(nc.vector.tensor_copy, w1_grouped[1], HM, w1b_raw[1][:], 44, HM)
+        for t0, t1 in ((0, 1), (1, 2), (2, PACK)):
             nc.vector.quantize_mx(
-                out=w1_codes[1][:, P * t : P * (t + 1)].bitcast(FP8X4),
-                scales=w1_scales[1][:, P * t : P * (t + 1)],
-                in_=w1_grouped[1][:, H * t : H * (t + 1)],
+                out=w1_codes[1][:, P * t0 : P * t1].bitcast(FP8X4),
+                scales=w1_scales[1][:, P * t0 : P * t1],
+                in_=w1_grouped[1][:, H * t0 : H * t1],
             )
         for c in range(CHUNKS):
             first_product(1, c, last_words[c])
@@ -149,7 +150,7 @@ def tile_picked_phpool_gelu_p_kernel(tc, x_words, x_scales, w1, w2, offs, out):
             largers.append(larger)
             for t in range(PACK):
                 reads = banks[c][t][:].rearrange("p (r v) -> p r v", r=2)
-                if (c, t) in ((0, 0), (CHUNKS - 1, PACK - 1)):
+                if (c, t) == (0, 0):
                     nc.vector.tensor_reduce(larger[:, t, :], reads.rearrange("p r v -> p v r"), mybir.AxisListType.X, MAX)
                 else:
                     first_read = keep.tile([P, CHUNK], F32, name="first_read%d%d" % (c, t))

@@ -105,8 +105,6 @@ def tile_picked_phpool_gelu_p_kernel(tc, x_words, x_scales, w1, w2, offs, out):
         for h in range(2):
             deal(nc.scalar.copy, w1_grouped[0], HM * h, w1a_raw[h][:], 0, HM)
 
-        banks = [[psum.tile([P, 2 * CHUNK], F32, name="y%d%d" % (c, t), tag="bank%d" % (4 * c + t)) for t in range(PACK)] for c in range(CHUNKS)]
-
         def first_product(z, c, words):
             for t in range(PACK):
                 nc.tensor.matmul_mx(
@@ -120,14 +118,30 @@ def tile_picked_phpool_gelu_p_kernel(tc, x_words, x_scales, w1, w2, offs, out):
                 )
 
         nc.vector.quantize_mx(out=w1_codes[0][:].bitcast(FP8X4), scales=w1_scales[0][:], in_=w1_grouped[0][:])
+        def warm_up(moving, tag):
+            scratch = psum.tile([P, 2 * CHUNK], F32, name="warm_" + tag, tag=tag)
+            nc.tensor.matmul_mx(
+                out=scratch[:],
+                lhsT=w1_codes[0][:, 0:P].bitcast(FP8X4),
+                lhsT_scale=w1_scales[0][:, 0:P],
+                rhs=moving[:].bitcast(FP8X4),
+                rhs_scale=w1_scales[0][:],
+                start=True,
+                stop=True,
+            )
+
         first_words = [gather_words(0, c, "scale_table_then_words" if c == 0 else "words01") for c in range(CHUNKS)]
+        for i, moving in enumerate((w1_codes[0], w1_codes[0], first_words[0], first_words[0])):
+            warm_up(moving, "bank%d" % i)
+        banks = [[psum.tile([P, 2 * CHUNK], F32, name="y%d%d" % (c, t), tag="bank%d" % (4 * c + t)) for t in range(PACK)] for c in range(CHUNKS)]
+
         for c in range(CHUNKS):
             first_product(0, c, first_words[c])
         last_words = [gather_words(1, c, "words1%d" % c) for c in range(CHUNKS)]
 
         deal(nc.scalar.copy, w1_grouped[1], 0, w1b_raw[0][:], 0, HM)
-        deal(nc.scalar.copy, w1_grouped[1], HM, w1b_raw[1][:], 0, 44)
-        deal(nc.vector.tensor_copy, w1_grouped[1], HM, w1b_raw[1][:], 44, HM)
+        deal(nc.scalar.copy, w1_grouped[1], HM, w1b_raw[1][:], 0, 18)
+        deal(nc.vector.tensor_copy, w1_grouped[1], HM, w1b_raw[1][:], 18, HM)
         for t0, t1 in ((0, 1), (1, 2), (2, PACK)):
             nc.vector.quantize_mx(
                 out=w1_codes[1][:, P * t0 : P * t1].bitcast(FP8X4),

@@ -22,7 +22,8 @@ CHUNK = 256
 CHUNKS = V // CHUNK
 LIST_ROWS = 16
 HALF = H // 2
-HM = HALF // PACK
+GROUPS = P // 4
+BEFORE_MOVES = 7 * T // 8
 
 
 def tile_picked_phpool_gelu_p_kernel(tc, x_words, x_scales, w1, w2, offs, out):
@@ -34,13 +35,16 @@ def tile_picked_phpool_gelu_p_kernel(tc, x_words, x_scales, w1, w2, offs, out):
         w1_rows = [w1[512 * z : 512 * (z + 1), :].rearrange("(p j) c -> p j c", j=PACK) for z in range(PASSES)]
         x_rows = [x_words[z].rearrange("p n t -> p (n t)").bitcast(I32) for z in range(PASSES)]
         word_table = [keep.tile([P, T], I32, name="word_table%d" % z) for z in range(PASSES)]
-        w1a_raw = [keep.tile([P, PACK, HALF], F32, name="w1a_raw%d" % h) for h in range(2)]
-        nc.sync.dma_start(w1a_raw[0][:], w1_rows[0][:, :, 0:HALF])
+        w1_raw = [[keep.tile([P, PACK, HALF], F32, name="w1_raw%d%d" % (z, h)) for h in range(2)] for z in range(PASSES)]
+
+        def load_w1(z, h):
+            nc.sync.dma_start(w1_raw[z][h][:], w1_rows[z][:, :, HALF * h : HALF * (h + 1)])
+
+        load_w1(0, 0)
         offsets = keep.tile([P, S // LIST_ROWS], U16, name="offsets")
         nc.sync.dma_start(offsets[:], offs)
-
-        scale_table = keep.tile([P, T], U8, name="scale_table", tag="scale_table_then_words", align_bytes=64)
-        nc.vector.memset(scale_table[:].bitcast(I32), 0)
+        scale_table = keep.tile([P, T], U8, name="scale_table", align_bytes=64)
+        nc.gpsimd.memset(scale_table[:].bitcast(I32), 0)
         for z in range(PASSES):
             for e in range(2):
                 nc.sync.dma_start(
@@ -52,9 +56,9 @@ def tile_picked_phpool_gelu_p_kernel(tc, x_words, x_scales, w1, w2, offs, out):
         warm = keep.tile([P, 1], F32, name="warm")
         nc.scalar.activation(warm[:], zero[:], GELU)
 
-        nc.sync.dma_start(w1a_raw[1][:], w1_rows[0][:, :, HALF:H])
+        load_w1(0, 1)
         nc.sync.dma_start(word_table[0][:], x_rows[0])
-        nc.sync.dma_start(word_table[1][:], x_rows[1])
+        nc.sync.dma_start(word_table[1][:, 0:BEFORE_MOVES], x_rows[1][:, 0:BEFORE_MOVES])
 
         def list_slice(c, r):
             first = (r * V + c * CHUNK) // LIST_ROWS
@@ -73,148 +77,173 @@ def tile_picked_phpool_gelu_p_kernel(tc, x_words, x_scales, w1, w2, offs, out):
                     planes[4 * z + 2 + e : P : 32, :].bitcast(I32),
                     planes[16 + 4 * z + e : P : 32, :].bitcast(I32),
                 )
-        w1b_raw = []
-        for h in range(2):
-            raw = keep.tile([P, PACK, HALF], F32, name="w1b_raw%d" % h)
-            nc.sync.dma_start(raw[:], w1_rows[1][:, :, HALF * h : HALF * (h + 1)])
-            w1b_raw.append(raw)
+        nc.sync.dma_start(word_table[1][:, BEFORE_MOVES:T], x_rows[1][:, BEFORE_MOVES:T])
+        load_w1(1, 0)
+        load_w1(1, 1)
         w2_raw = keep.tile([P, PACK, N], F32, name="w2_raw")
-        nc.sync.dma_start(w2_raw[:], w2.rearrange("(p j) n -> p j n", j=PACK))
-
+        w2_rows = w2.rearrange("(g t i) n -> t g i n", t=PACK, i=4)
+        for t in range(PACK):
+            nc.sync.dma_start(w2_raw[:, t, :], w2_rows[t])
 
         w1_codes = [keep.tile([P, H], U32, name="w1_codes%d" % z, align_bytes=64) for z in range(PASSES)]
         w1_scales = [keep.tile([P, H], U8, name="w1_scales%d" % z, align_bytes=64) for z in range(PASSES)]
-
-        def deal(copy, grouped, m_first, raw, m0, m1):
-            copy(
-                grouped[:].rearrange("p (t m j) -> p m t j", t=PACK, j=PACK)[:, m_first + m0 : m_first + m1],
-                raw.rearrange("p j (m t) -> p m t j", t=PACK)[:, m0:m1],
-            )
-
-        def gather_words(z, c, tag):
-            words = keep.tile([P, 2 * CHUNK], U32, name="picked_words%d%d" % (z, c), tag=tag, align_bytes=64)
-            for r in range(2):
-                nc.vector.tensor_copy(
-                    words[:, r * CHUNK : (r + 1) * CHUNK], word_table[z][:].bitcast(U32).indirect(list_slice(c, r))
-                )
-            return words
-
         w1_grouped = [
             keep.tile([P, PACK * H], BF16, name="w1_grouped%d" % z, tag="grouped%d" % z, align_bytes=64) for z in range(PASSES)
         ]
-        for h in range(2):
-            deal(nc.scalar.copy, w1_grouped[0], HM * h, w1a_raw[h][:], 0, HM)
 
-        def first_product(z, c, words):
-            for t in range(PACK):
-                nc.tensor.matmul_mx(
-                    out=banks[c][t][:],
-                    lhsT=w1_codes[z][:, P * t : P * (t + 1)].bitcast(FP8X4),
-                    lhsT_scale=w1_scales[z][:, P * t : P * (t + 1)],
-                    rhs=words[:].bitcast(FP8X4),
-                    rhs_scale=planes[4 * z : P, 2 * CHUNK * c : 2 * CHUNK * (c + 1)],
-                    start=(z == 0),
-                    stop=(z == PASSES - 1),
+        def deal(z, h, t0, t1, copy=nc.scalar.copy):
+            copy(
+                w1_grouped[z][:].rearrange("p (t h g i j) -> p h g t j i", t=PACK, h=2, i=4, j=PACK)[:, h, :, t0:t1],
+                w1_raw[z][h][:].rearrange("p j (g t i) -> p g t j i", t=PACK, i=4)[:, :, t0:t1],
+            )
+
+        def quantize_w1(z, t0, t1):
+            nc.vector.quantize_mx(
+                out=w1_codes[z][:, P * t0 : P * t1].bitcast(FP8X4),
+                scales=w1_scales[z][:, P * t0 : P * t1],
+                in_=w1_grouped[z][:, H * t0 : H * t1],
+            )
+
+        def gather_words(words, z, c):
+            for r in range(2):
+                nc.vector.tensor_copy(
+                    words[:, (2 * c + r) * CHUNK : (2 * c + r + 1) * CHUNK], word_table[z][:].bitcast(U32).indirect(list_slice(c, r))
                 )
 
-        nc.vector.quantize_mx(out=w1_codes[0][:].bitcast(FP8X4), scales=w1_scales[0][:], in_=w1_grouped[0][:])
-        def warm_up(moving, tag):
-            scratch = psum.tile([P, 2 * CHUNK], F32, name="warm_" + tag, tag=tag)
+        warm_banks = [psum.tile([P, 2 * CHUNK], F32, name="warm%d" % i, tag="bank%d" % i) for i in range(2)]
+        banks = [[psum.tile([P, 2 * CHUNK], F32, name="y%d%d" % (c, t), tag="bank%d" % (4 * c + t)) for t in range(PACK)] for c in range(CHUNKS)]
+
+        def first_product(z, words):
+            for c in range(CHUNKS):
+                cols = slice(2 * CHUNK * c, 2 * CHUNK * (c + 1))
+                for t in range(PACK):
+                    nc.tensor.matmul_mx(
+                        out=banks[c][t][:],
+                        lhsT=w1_codes[z][:, P * t : P * (t + 1)].bitcast(FP8X4),
+                        lhsT_scale=w1_scales[z][:, P * t : P * (t + 1)],
+                        rhs=words[:, cols].bitcast(FP8X4),
+                        rhs_scale=planes[4 * z : P, cols],
+                        start=(z == 0),
+                        stop=(z == PASSES - 1),
+                    )
+
+        deal(0, 0, 0, PACK)
+        deal(0, 1, 0, PACK)
+        quantize_w1(0, 0, PACK)
+        for scratch in warm_banks:
             nc.tensor.matmul_mx(
                 out=scratch[:],
                 lhsT=w1_codes[0][:, 0:P].bitcast(FP8X4),
                 lhsT_scale=w1_scales[0][:, 0:P],
-                rhs=moving[:].bitcast(FP8X4),
+                rhs=w1_codes[0][:].bitcast(FP8X4),
                 rhs_scale=w1_scales[0][:],
                 start=True,
                 stop=True,
             )
-
-        first_words = [gather_words(0, c, "scale_table_then_words" if c == 0 else "words01") for c in range(CHUNKS)]
-        for i, moving in enumerate((w1_codes[0], w1_codes[0], first_words[0], first_words[0])):
-            warm_up(moving, "bank%d" % i)
-        banks = [[psum.tile([P, 2 * CHUNK], F32, name="y%d%d" % (c, t), tag="bank%d" % (4 * c + t)) for t in range(PACK)] for c in range(CHUNKS)]
-
+        first_words = keep.tile([P, S], U32, name="first_words", tag="grouped0", align_bytes=64)
         for c in range(CHUNKS):
-            first_product(0, c, first_words[c])
-        last_words = [gather_words(1, c, "words1%d" % c) for c in range(CHUNKS)]
-
-        deal(nc.scalar.copy, w1_grouped[1], 0, w1b_raw[0][:], 0, HM)
-        deal(nc.scalar.copy, w1_grouped[1], HM, w1b_raw[1][:], 0, 18)
-        deal(nc.vector.tensor_copy, w1_grouped[1], HM, w1b_raw[1][:], 18, HM)
-        for t0, t1 in ((0, 1), (1, 2), (2, PACK)):
-            nc.vector.quantize_mx(
-                out=w1_codes[1][:, P * t0 : P * t1].bitcast(FP8X4),
-                scales=w1_scales[1][:, P * t0 : P * t1],
-                in_=w1_grouped[1][:, H * t0 : H * t1],
-            )
+            gather_words(first_words, 0, c)
+        first_product(0, first_words)
+        last_words = keep.tile([P, S], U32, name="last_words", align_bytes=64)
         for c in range(CHUNKS):
-            first_product(1, c, last_words[c])
+            gather_words(last_words, 1, c)
 
-        w2_grouped = keep.tile([P, PACK * N], BF16, name="w2_grouped", align_bytes=64)
-        w2_codes = keep.tile([P, N], U32, name="w2_codes", align_bytes=64)
+        deal(1, 0, 0, PACK)
+        for t in range(PACK - 1):
+            deal(1, 1, t, t + 1)
+        quantize_w1(1, 0, 1)
+        deal(1, 1, PACK - 1, PACK, nc.vector.tensor_copy)
+        for t in range(1, PACK):
+            quantize_w1(1, t, t + 1)
+        first_product(1, last_words)
+
+        w2_grouped = keep.tile([P, PACK * N], BF16, name="w2_grouped", tag="grouped1", align_bytes=64)
         w2_scales = keep.tile([P, N], U8, name="w2_scales", align_bytes=64)
-        nc.scalar.copy(
-            w2_grouped[:].rearrange("p (c i j) -> p c j i", i=4, j=PACK), w2_raw[:].rearrange("p j (c i) -> p c j i", i=4)
+        nc.gpsimd.tensor_scalar(
+            w2_grouped[:].rearrange("p (n j) -> p n j", j=PACK),
+            w2_raw[:].rearrange("p j n -> p n j"),
+            1.0,
+            0.0,
+            mybir.AluOpType.mult,
+            mybir.AluOpType.add,
         )
 
-        largers = []
-        for c in range(CHUNKS):
-            larger = keep.tile([P, PACK, CHUNK], F32, name="larger%d" % c)
-            largers.append(larger)
-            for t in range(PACK):
-                reads = banks[c][t][:].rearrange("p (r v) -> p r v", r=2)
-                if (c, t) == (0, 0):
-                    nc.vector.tensor_reduce(larger[:, t, :], reads.rearrange("p r v -> p v r"), mybir.AxisListType.X, MAX)
-                else:
-                    first_read = keep.tile([P, CHUNK], F32, name="first_read%d%d" % (c, t))
-                    nc.scalar.copy(first_read[:], reads[:, 0, :])
-                    nc.vector.tensor_tensor(larger[:, t, :], first_read[:], reads[:, 1, :], MAX)
-                if (c, t) == (0, 0):
-                    nc.vector.quantize_mx(out=w2_codes[:].bitcast(FP8X4), scales=w2_scales[:], in_=w2_grouped[:])
+        largers = [keep.tile([P, PACK, CHUNK], F32, name="larger%d" % c) for c in range(CHUNKS)]
+
+        def larger_of(c, t, shared):
+            reads = banks[c][t][:].rearrange("p (r v) -> p r v", r=2)
+            if shared:
+                first_read = keep.tile([P, CHUNK], F32, name="first_read%d%d" % (c, t), tag="first_read%d%d" % (c, t), align_bytes=64)
+                nc.scalar.copy(first_read[:], reads[:, 0, :])
+                nc.vector.tensor_tensor(largers[c][:, t, :], first_read[:], reads[:, 1, :], MAX)
+            else:
+                nc.vector.tensor_reduce(largers[c][:, t, :], reads.rearrange("p r v -> p v r"), mybir.AxisListType.X, MAX)
 
         pieces = [(0, 0, 256), (1, 0, 128), (1, 128, 128)]
-        z_grouped = []
-        for c, v0, n in pieces:
-            grouped = keep.tile([P, PACK * n], BF16, name="z_grouped%d_%d" % (c, v0), align_bytes=64)
+        z_grouped = [keep.tile([P, PACK * n], BF16, name="z_grouped%d" % i, align_bytes=64) for i, (c, v0, n) in enumerate(pieces)]
+
+        def gelu(i):
+            c, v0, n = pieces[i]
             nc.scalar.activation(
-                grouped[:].rearrange("p (c i t) -> p c t i", i=4, t=PACK),
+                z_grouped[i][:].rearrange("p (c i t) -> p c t i", i=4, t=PACK),
                 largers[c][:, :, v0 : v0 + n].rearrange("p t (c i) -> p c t i", i=4),
                 GELU,
             )
-            z_grouped.append(grouped)
 
         out_rows = out.rearrange("(h p) v -> p h v", p=P)
-        for i, (c, v0, n) in enumerate(pieces):
-            z_codes = keep.tile([P, n], U32, name="z_codes%d" % i, align_bytes=64)
+
+        chunk_codes = []
+
+        def second_product(i, tags):
+            c, v0, n = pieces[i]
+            if v0 == 0:
+                chunk_codes.append(keep.tile([P, CHUNK], U32, name="z_codes%d" % c, tag="z_codes", align_bytes=64))
+            z_codes = chunk_codes[c][:, v0 : v0 + n]
             z_scales = keep.tile([P, n], U8, name="z_scales%d" % i, align_bytes=64)
-            nc.vector.quantize_mx(out=z_codes[:].bitcast(FP8X4), scales=z_scales[:], in_=z_grouped[i][:])
-            if i == 1:
-                both = psum.tile([P, 2, n], F32, name="acc%d" % i, tag="bank2")
+            nc.vector.quantize_mx(out=z_codes.bitcast(FP8X4), scales=z_scales[:], in_=z_grouped[i][:])
+            if len(tags) == 1:
+                both = psum.tile([P, 2, n], F32, name="acc%d" % i, tag=tags[0])
                 accs = [both[:, h, :] for h in range(2)]
             else:
-                accs = [psum.tile([P, n], F32, name="acc%d_%d" % (i, h), tag="bank%d" % (3 * i // 2 + h))[:] for h in range(2)]
+                both = None
+                accs = [psum.tile([P, n], F32, name="acc%d_%d" % (i, h), tag=tags[h])[:] for h in range(2)]
             for h in range(2):
                 nc.tensor.matmul_mx(
                     out=accs[h],
                     lhsT=w2_codes[:, P * h : P * (h + 1)].bitcast(FP8X4),
                     lhsT_scale=w2_scales[:, P * h : P * (h + 1)],
-                    rhs=z_codes[:].bitcast(FP8X4),
+                    rhs=z_codes.bitcast(FP8X4),
                     rhs_scale=z_scales[:],
                     start=True,
                     stop=True,
                 )
+            return both, accs
+
+        def store(i, copy, both, accs):
+            c, v0, n = pieces[i]
             cols = slice(c * CHUNK + v0, c * CHUNK + v0 + n)
-            if i == 0:
-                for h, copy in enumerate((nc.vector.tensor_copy, nc.scalar.copy)):
-                    half = keep.tile([P, n], F32, name="result0_%d" % h)
-                    copy(half[:], accs[h])
-                    nc.sync.dma_start(out_rows[:, h, cols], half[:])
+            result = keep.tile([P, 2, n], F32, name="result%d" % i)
+            if both is not None:
+                copy(result[:], both[:])
             else:
-                result = keep.tile([P, 2, n], F32, name="result%d" % i)
-                if i == 1:
-                    nc.vector.tensor_copy(result[:], both[:])
-                else:
-                    nc.vector.tensor_copy(result[:, 0, :], accs[0])
-                    nc.scalar.copy(result[:, 1, :], accs[1])
-                nc.sync.dma_start(out_rows[:, :, cols], result[:])
+                nc.vector.tensor_copy(result[:, 0, :], accs[0])
+                nc.scalar.copy(result[:, 1, :], accs[1])
+            nc.sync.dma_start(out_rows[:, :, cols], result[:])
+
+        for t in range(PACK):
+            larger_of(0, t, True)
+        larger_of(1, 0, True)
+        larger_of(1, 1, True)
+        larger_of(1, 2, True)
+        larger_of(1, 3, False)
+        gelu(0)
+        w2_codes = keep.tile([P, N], U32, name="w2_codes", tag="first_read11", align_bytes=64)
+        nc.vector.quantize_mx(out=w2_codes[:].bitcast(FP8X4), scales=w2_scales[:], in_=w2_grouped[:])
+        first = second_product(0, ["bank0"])
+        gelu(1)
+        gelu(2)
+        second = second_product(1, ["bank1"])
+        store(0, nc.scalar.copy, *first)
+        third = second_product(2, ["bank2", "bank3"])
+        store(1, nc.vector.tensor_copy, *second)
+        store(2, None, *third)

@@ -22,8 +22,7 @@ CHUNK = 256
 CHUNKS = V // CHUNK
 LIST_ROWS = 16
 HALF = H // 2
-GROUPS = P // 4
-BEFORE_MOVES = 7 * T // 8
+GROUPS = 16
 
 
 def tile_picked_phpool_gelu_p_kernel(tc, x_words, x_scales, w1, w2, offs, out):
@@ -35,22 +34,19 @@ def tile_picked_phpool_gelu_p_kernel(tc, x_words, x_scales, w1, w2, offs, out):
         w1_rows = [w1[512 * z : 512 * (z + 1), :].rearrange("(p j) c -> p j c", j=PACK) for z in range(PASSES)]
         x_rows = [x_words[z].rearrange("p n t -> p (n t)").bitcast(I32) for z in range(PASSES)]
         word_table = [keep.tile([P, T], I32, name="word_table%d" % z) for z in range(PASSES)]
-        w1_raw = [[keep.tile([P, PACK, HALF], F32, name="w1_raw%d%d" % (z, h)) for h in range(2)] for z in range(PASSES)]
+        w1_raw = [[keep.tile([P, PACK, HALF], F32, name="w1_raw0%d" % h)[:] for h in range(2)]]
 
         def load_w1(z, h):
-            nc.sync.dma_start(w1_raw[z][h][:], w1_rows[z][:, :, HALF * h : HALF * (h + 1)])
+            nc.sync.dma_start(w1_raw[z][h], w1_rows[z][:, :, HALF * h : HALF * (h + 1)])
 
         load_w1(0, 0)
         offsets = keep.tile([P, S // LIST_ROWS], U16, name="offsets")
         nc.sync.dma_start(offsets[:], offs)
-        scale_table = keep.tile([P, T], U8, name="scale_table", align_bytes=64)
-        nc.gpsimd.memset(scale_table[:].bitcast(I32), 0)
-        for z in range(PASSES):
-            for e in range(2):
-                nc.sync.dma_start(
-                    scale_table[4 * z + e : P : LIST_ROWS, :].bitcast(I32),
-                    x_scales[z, e : 16 : 2, :].bitcast(I32),
-                )
+        scale_table = keep.tile([P, T], U8, name="scale_table", tag="scale_table", align_bytes=64)
+        nc.vector.memset(scale_table[:].bitcast(I32), 0)
+        nc.sync.dma_start(scale_table[0:P:4, :].bitcast(I32), x_scales.rearrange("z q c -> q z c").bitcast(I32))
+        planes = keep.tile([P, PASSES, S], U8, name="planes", align_bytes=64)
+        nc.gpsimd.memset(planes[:].rearrange("p z s -> p (z s)").bitcast(I32), 0)
         zero = keep.tile([P, 1], F32, name="zero")
         nc.vector.memset(zero[:], 0.0)
         warm = keep.tile([P, 1], F32, name="warm")
@@ -58,29 +54,25 @@ def tile_picked_phpool_gelu_p_kernel(tc, x_words, x_scales, w1, w2, offs, out):
 
         load_w1(0, 1)
         nc.sync.dma_start(word_table[0][:], x_rows[0])
-        nc.sync.dma_start(word_table[1][:, 0:BEFORE_MOVES], x_rows[1][:, 0:BEFORE_MOVES])
+        nc.sync.dma_start(word_table[1][:], x_rows[1])
 
-        def list_slice(c, r):
-            first = (r * V + c * CHUNK) // LIST_ROWS
-            return offsets[:, first : first + CHUNK // LIST_ROWS]
+        def gather(picked, table):
+            for first, count, at in ((CHUNK, 2 * CHUNK, CHUNK), (0, CHUNK, 3 * CHUNK), (3 * CHUNK, CHUNK, 0)):
+                entries = offsets[:, first // LIST_ROWS : (first + count) // LIST_ROWS]
+                nc.vector.tensor_copy(picked[:, at : at + count], table.indirect(entries))
 
         picked_scales = keep.tile([P, S], U8, name="picked_scales", align_bytes=64)
-        nc.vector.tensor_copy(picked_scales[:], scale_table[:].indirect(offsets[:]))
-        planes = keep.tile([P, S], U8, name="planes", align_bytes=64)
-        nc.vector.tensor_copy(
-            planes[:].bitcast(I32).rearrange("p (c r w) -> p c r w", c=CHUNKS, r=2),
-            picked_scales[:].bitcast(I32).rearrange("p (r c w) -> p c r w", c=CHUNKS, r=2),
-        )
-        for z in range(PASSES):
-            for e in range(2):
-                nc.sync.dma_start(
-                    planes[4 * z + 2 + e : P : 32, :].bitcast(I32),
-                    planes[16 + 4 * z + e : P : 32, :].bitcast(I32),
-                )
-        nc.sync.dma_start(word_table[1][:, BEFORE_MOVES:T], x_rows[1][:, BEFORE_MOVES:T])
+        gather(picked_scales, scale_table[:])
+        for q in range(4):
+            nc.sync.dma_start(
+                planes[32 * q : 32 * q + 4].bitcast(I32),
+                picked_scales[32 * q : 32 * q + 32 : 4, :].bitcast(I32),
+            )
+        late = keep.tile([P, 3, PACK, HALF], F32, name="late", tag="scale_table", align_bytes=64)
+        w1_raw.append([late[:, h] for h in range(2)])
         load_w1(1, 0)
         load_w1(1, 1)
-        w2_raw = keep.tile([P, PACK, N], F32, name="w2_raw")
+        w2_raw = late[:, 2]
         w2_rows = w2.rearrange("(g t i) n -> t g i n", t=PACK, i=4)
         for t in range(PACK):
             nc.sync.dma_start(w2_raw[:, t, :], w2_rows[t])
@@ -93,8 +85,8 @@ def tile_picked_phpool_gelu_p_kernel(tc, x_words, x_scales, w1, w2, offs, out):
 
         def deal(z, h, t0, t1, copy=nc.scalar.copy):
             copy(
-                w1_grouped[z][:].rearrange("p (t h g i j) -> p h g t j i", t=PACK, h=2, i=4, j=PACK)[:, h, :, t0:t1],
-                w1_raw[z][h][:].rearrange("p j (g t i) -> p g t j i", t=PACK, i=4)[:, :, t0:t1],
+                w1_grouped[z][:].rearrange("p (t g i j) -> p g t j i", t=PACK, i=4, j=PACK)[:, GROUPS * h : GROUPS * (h + 1), t0:t1],
+                w1_raw[z][h].rearrange("p j (g t i) -> p g t j i", t=PACK, i=4)[:, :, t0:t1],
             )
 
         def quantize_w1(z, t0, t1):
@@ -104,49 +96,41 @@ def tile_picked_phpool_gelu_p_kernel(tc, x_words, x_scales, w1, w2, offs, out):
                 in_=w1_grouped[z][:, H * t0 : H * t1],
             )
 
-        def gather_words(words, z, c):
-            for r in range(2):
-                nc.vector.tensor_copy(
-                    words[:, (2 * c + r) * CHUNK : (2 * c + r + 1) * CHUNK], word_table[z][:].bitcast(U32).indirect(list_slice(c, r))
-                )
-
         warm_banks = [psum.tile([P, 2 * CHUNK], F32, name="warm%d" % i, tag="bank%d" % i) for i in range(2)]
         banks = [[psum.tile([P, 2 * CHUNK], F32, name="y%d%d" % (c, t), tag="bank%d" % (4 * c + t)) for t in range(PACK)] for c in range(CHUNKS)]
 
         def first_product(z, words):
             for c in range(CHUNKS):
-                cols = slice(2 * CHUNK * c, 2 * CHUNK * (c + 1))
+                cols = slice(2 * CHUNK * (1 - c), 2 * CHUNK * (2 - c))
                 for t in range(PACK):
                     nc.tensor.matmul_mx(
                         out=banks[c][t][:],
                         lhsT=w1_codes[z][:, P * t : P * (t + 1)].bitcast(FP8X4),
                         lhsT_scale=w1_scales[z][:, P * t : P * (t + 1)],
                         rhs=words[:, cols].bitcast(FP8X4),
-                        rhs_scale=planes[4 * z : P, cols],
+                        rhs_scale=planes[:, z, cols],
                         start=(z == 0),
                         stop=(z == PASSES - 1),
                     )
 
-        deal(0, 0, 0, PACK)
-        deal(0, 1, 0, PACK)
+        for h in range(2):
+            deal(0, h, 0, PACK)
         quantize_w1(0, 0, PACK)
+        first_words = keep.tile([P, S], U32, name="first_words", tag="grouped0", align_bytes=64)
+        gather(first_words, word_table[0][:].bitcast(U32))
         for scratch in warm_banks:
             nc.tensor.matmul_mx(
                 out=scratch[:],
                 lhsT=w1_codes[0][:, 0:P].bitcast(FP8X4),
                 lhsT_scale=w1_scales[0][:, 0:P],
-                rhs=w1_codes[0][:].bitcast(FP8X4),
+                rhs=first_words[:, CHUNK : 3 * CHUNK].bitcast(FP8X4),
                 rhs_scale=w1_scales[0][:],
                 start=True,
                 stop=True,
             )
-        first_words = keep.tile([P, S], U32, name="first_words", tag="grouped0", align_bytes=64)
-        for c in range(CHUNKS):
-            gather_words(first_words, 0, c)
         first_product(0, first_words)
         last_words = keep.tile([P, S], U32, name="last_words", align_bytes=64)
-        for c in range(CHUNKS):
-            gather_words(last_words, 1, c)
+        gather(last_words, word_table[1][:].bitcast(U32))
 
         deal(1, 0, 0, PACK)
         for t in range(PACK - 1):
@@ -161,7 +145,7 @@ def tile_picked_phpool_gelu_p_kernel(tc, x_words, x_scales, w1, w2, offs, out):
         w2_scales = keep.tile([P, N], U8, name="w2_scales", align_bytes=64)
         nc.gpsimd.tensor_scalar(
             w2_grouped[:].rearrange("p (n j) -> p n j", j=PACK),
-            w2_raw[:].rearrange("p j n -> p n j"),
+            w2_raw.rearrange("p j n -> p n j"),
             1.0,
             0.0,
             mybir.AluOpType.mult,
@@ -179,7 +163,7 @@ def tile_picked_phpool_gelu_p_kernel(tc, x_words, x_scales, w1, w2, offs, out):
             else:
                 nc.vector.tensor_reduce(largers[c][:, t, :], reads.rearrange("p r v -> p v r"), mybir.AxisListType.X, MAX)
 
-        pieces = [(0, 0, 256), (1, 0, 128), (1, 128, 128)]
+        pieces = [(c, v0, P) for c in range(CHUNKS) for v0 in range(0, CHUNK, P)]
         z_grouped = [keep.tile([P, PACK * n], BF16, name="z_grouped%d" % i, align_bytes=64) for i, (c, v0, n) in enumerate(pieces)]
 
         def gelu(i):
@@ -192,13 +176,9 @@ def tile_picked_phpool_gelu_p_kernel(tc, x_words, x_scales, w1, w2, offs, out):
 
         out_rows = out.rearrange("(h p) v -> p h v", p=P)
 
-        chunk_codes = []
-
         def second_product(i, tags):
             c, v0, n = pieces[i]
-            if v0 == 0:
-                chunk_codes.append(keep.tile([P, CHUNK], U32, name="z_codes%d" % c, tag="z_codes", align_bytes=64))
-            z_codes = chunk_codes[c][:, v0 : v0 + n]
+            z_codes = all_codes[:, c * CHUNK + v0 : c * CHUNK + v0 + n]
             z_scales = keep.tile([P, n], U8, name="z_scales%d" % i, align_bytes=64)
             nc.vector.quantize_mx(out=z_codes.bitcast(FP8X4), scales=z_scales[:], in_=z_grouped[i][:])
             if len(tags) == 1:
@@ -237,13 +217,17 @@ def tile_picked_phpool_gelu_p_kernel(tc, x_words, x_scales, w1, w2, offs, out):
         larger_of(1, 2, True)
         larger_of(1, 3, False)
         gelu(0)
-        w2_codes = keep.tile([P, N], U32, name="w2_codes", tag="first_read11", align_bytes=64)
+        w2_codes = keep.tile([P, N], U32, name="w2_codes", tag="first_read03", align_bytes=64)
         nc.vector.quantize_mx(out=w2_codes[:].bitcast(FP8X4), scales=w2_scales[:], in_=w2_grouped[:])
-        first = second_product(0, ["bank0"])
+        all_codes = keep.tile([P, V], U32, name="all_codes", tag="grouped1", align_bytes=64)
+        results = [second_product(0, ["bank0"])]
         gelu(1)
+        results.append(second_product(1, ["bank1"]))
         gelu(2)
-        second = second_product(1, ["bank1"])
-        store(0, nc.scalar.copy, *first)
-        third = second_product(2, ["bank2", "bank3"])
-        store(1, nc.vector.tensor_copy, *second)
-        store(2, None, *third)
+        results.append(second_product(2, ["bank2"]))
+        gelu(3)
+        results.append(second_product(3, ["bank3", "bank4"]))
+        store(0, nc.scalar.copy, *results[0])
+        store(1, nc.scalar.copy, *results[1])
+        store(2, nc.vector.tensor_copy, *results[2])
+        store(3, None, *results[3])

@@ -17,12 +17,17 @@ MAX = mybir.AluOpType.max
 
 P = 128
 PACK = 4
+LINE = 4
 PASSES = K // (P * PACK)
+LIST_ROWS = 16
 CHUNK = 256
 CHUNKS = V // CHUNK
-LIST_ROWS = 16
+PIECE = 128
 HALF = H // 2
-GROUPS = 16
+GROUPS = HALF // (PACK * LINE)
+QUADRANT = 32
+WARM_UPS = 2
+EARLY_BANKS = CHUNKS * PACK - 1
 
 
 def tile_picked_phpool_gelu_p_kernel(tc, x_words, x_scales, w1, w2, offs, out):
@@ -31,8 +36,8 @@ def tile_picked_phpool_gelu_p_kernel(tc, x_words, x_scales, w1, w2, offs, out):
         keep = ctx.enter_context(tc.tile_pool(name="keep", bufs=1))
         psum = ctx.enter_context(tc.psum_pool(name="psum", bufs=1))
 
-        w1_rows = [w1[512 * z : 512 * (z + 1), :].rearrange("(p j) c -> p j c", j=PACK) for z in range(PASSES)]
-        x_rows = [x_words[z].rearrange("p n t -> p (n t)").bitcast(I32) for z in range(PASSES)]
+        w1_rows = [w1[P * PACK * z : P * PACK * (z + 1), :].rearrange("(p j) c -> p j c", j=PACK) for z in range(PASSES)]
+        x_rows = [x_words[z].rearrange("p n j -> p (n j)").bitcast(I32) for z in range(PASSES)]
         word_table = [keep.tile([P, T], I32, name="word_table%d" % z) for z in range(PASSES)]
         w1_raw = [[keep.tile([P, PACK, HALF], F32, name="w1_raw0%d" % h)[:] for h in range(2)]]
 
@@ -49,12 +54,12 @@ def tile_picked_phpool_gelu_p_kernel(tc, x_words, x_scales, w1, w2, offs, out):
         nc.gpsimd.memset(planes[:].rearrange("p z s -> p (z s)").bitcast(I32), 0)
         zero = keep.tile([P, 1], F32, name="zero")
         nc.vector.memset(zero[:], 0.0)
-        warm = keep.tile([P, 1], F32, name="warm")
-        nc.scalar.activation(warm[:], zero[:], GELU)
+        no_bias = keep.tile([P, 1], F32, name="no_bias")
+        nc.scalar.activation(no_bias[:], zero[:], GELU)
 
         load_w1(0, 1)
-        nc.sync.dma_start(word_table[0][:], x_rows[0])
-        nc.sync.dma_start(word_table[1][:], x_rows[1])
+        for z in range(PASSES):
+            nc.sync.dma_start(word_table[z][:], x_rows[z])
 
         def gather(picked, table):
             for first, count, at in ((CHUNK, 2 * CHUNK, CHUNK), (0, CHUNK, 3 * CHUNK), (3 * CHUNK, CHUNK, 0)):
@@ -63,17 +68,17 @@ def tile_picked_phpool_gelu_p_kernel(tc, x_words, x_scales, w1, w2, offs, out):
 
         picked_scales = keep.tile([P, S], U8, name="picked_scales", align_bytes=64)
         gather(picked_scales, scale_table[:])
-        for q in range(4):
+        for q in range(P // QUADRANT):
             nc.sync.dma_start(
-                planes[32 * q : 32 * q + 4].bitcast(I32),
-                picked_scales[32 * q : 32 * q + 32 : 4, :].bitcast(I32),
+                planes[QUADRANT * q : QUADRANT * q + 4].bitcast(I32),
+                picked_scales[QUADRANT * q : QUADRANT * (q + 1) : 4, :].bitcast(I32),
             )
         late = keep.tile([P, 3, PACK, HALF], F32, name="late", tag="scale_table", align_bytes=64)
         w1_raw.append([late[:, h] for h in range(2)])
         load_w1(1, 0)
         load_w1(1, 1)
         w2_raw = late[:, 2]
-        w2_rows = w2.rearrange("(g t i) n -> t g i n", t=PACK, i=4)
+        w2_rows = w2.rearrange("(g t u) n -> t g u n", t=PACK, u=LINE)
         for t in range(PACK):
             nc.sync.dma_start(w2_raw[:, t, :], w2_rows[t])
 
@@ -83,10 +88,10 @@ def tile_picked_phpool_gelu_p_kernel(tc, x_words, x_scales, w1, w2, offs, out):
             keep.tile([P, PACK * H], BF16, name="w1_grouped%d" % z, tag="grouped%d" % z, align_bytes=64) for z in range(PASSES)
         ]
 
-        def deal(z, h, t0, t1, copy=nc.scalar.copy):
+        def deal(z, h, t0, t1, copy):
             copy(
-                w1_grouped[z][:].rearrange("p (t g i j) -> p g t j i", t=PACK, i=4, j=PACK)[:, GROUPS * h : GROUPS * (h + 1), t0:t1],
-                w1_raw[z][h].rearrange("p j (g t i) -> p g t j i", t=PACK, i=4)[:, :, t0:t1],
+                w1_grouped[z][:].rearrange("p (t g u j) -> p g t j u", t=PACK, u=LINE, j=PACK)[:, GROUPS * h : GROUPS * (h + 1), t0:t1],
+                w1_raw[z][h].rearrange("p j (g t u) -> p g t j u", t=PACK, u=LINE)[:, :, t0:t1],
             )
 
         def quantize_w1(z, t0, t1):
@@ -96,29 +101,33 @@ def tile_picked_phpool_gelu_p_kernel(tc, x_words, x_scales, w1, w2, offs, out):
                 in_=w1_grouped[z][:, H * t0 : H * t1],
             )
 
-        warm_banks = [psum.tile([P, 2 * CHUNK], F32, name="warm%d" % i, tag="bank%d" % i) for i in range(2)]
-        banks = [[psum.tile([P, 2 * CHUNK], F32, name="y%d%d" % (c, t), tag="bank%d" % (4 * c + t)) for t in range(PACK)] for c in range(CHUNKS)]
+        scratch_banks = [psum.tile([P, 2 * CHUNK], F32, name="scratch%d" % i, tag="bank%d" % i) for i in range(WARM_UPS)]
+        banks = [
+            [psum.tile([P, 2 * CHUNK], F32, name="y%d%d" % (c, t), tag="bank%d" % (PACK * c + t)) for t in range(PACK)]
+            for c in range(CHUNKS)
+        ]
 
-        def first_product(z, words):
-            for c in range(CHUNKS):
-                cols = slice(2 * CHUNK * (1 - c), 2 * CHUNK * (2 - c))
-                for t in range(PACK):
-                    nc.tensor.matmul_mx(
-                        out=banks[c][t][:],
-                        lhsT=w1_codes[z][:, P * t : P * (t + 1)].bitcast(FP8X4),
-                        lhsT_scale=w1_scales[z][:, P * t : P * (t + 1)],
-                        rhs=words[:, cols].bitcast(FP8X4),
-                        rhs_scale=planes[:, z, cols],
-                        start=(z == 0),
-                        stop=(z == PASSES - 1),
-                    )
+        def one_pass(z, c, t, start):
+            cols = slice(2 * CHUNK * (CHUNKS - 1 - c), 2 * CHUNK * (CHUNKS - c))
+            nc.tensor.matmul_mx(
+                out=banks[c][t][:],
+                lhsT=w1_codes[z][:, P * t : P * (t + 1)].bitcast(FP8X4),
+                lhsT_scale=w1_scales[z][:, P * t : P * (t + 1)],
+                rhs=picked_words[z][:, cols].bitcast(FP8X4),
+                rhs_scale=planes[:, z, cols],
+                start=start,
+                stop=not start,
+            )
+
+        all_banks = [(c, t) for c in range(CHUNKS) for t in range(PACK)]
+        early_banks, late_banks = all_banks[:EARLY_BANKS], all_banks[EARLY_BANKS:]
 
         for h in range(2):
-            deal(0, h, 0, PACK)
+            deal(0, h, 0, PACK, nc.scalar.copy)
         quantize_w1(0, 0, PACK)
         first_words = keep.tile([P, S], U32, name="first_words", tag="grouped0", align_bytes=64)
         gather(first_words, word_table[0][:].bitcast(U32))
-        for scratch in warm_banks:
+        for scratch in scratch_banks:
             nc.tensor.matmul_mx(
                 out=scratch[:],
                 lhsT=w1_codes[0][:, 0:P].bitcast(FP8X4),
@@ -128,24 +137,31 @@ def tile_picked_phpool_gelu_p_kernel(tc, x_words, x_scales, w1, w2, offs, out):
                 start=True,
                 stop=True,
             )
-        first_product(0, first_words)
+        picked_words = [first_words]
+        for c, t in early_banks:
+            one_pass(0, c, t, True)
         last_words = keep.tile([P, S], U32, name="last_words", align_bytes=64)
         gather(last_words, word_table[1][:].bitcast(U32))
 
-        deal(1, 0, 0, PACK)
+        deal(1, 0, 0, PACK, nc.scalar.copy)
         for t in range(PACK - 1):
-            deal(1, 1, t, t + 1)
+            deal(1, 1, t, t + 1, nc.scalar.copy)
         quantize_w1(1, 0, 1)
         deal(1, 1, PACK - 1, PACK, nc.vector.tensor_copy)
         for t in range(1, PACK):
             quantize_w1(1, t, t + 1)
-        first_product(1, last_words)
+        picked_words.append(last_words)
+        for c, t in early_banks:
+            one_pass(1, c, t, False)
+        for c, t in late_banks:
+            one_pass(1, c, t, True)
+            one_pass(0, c, t, False)
 
         w2_grouped = keep.tile([P, PACK * N], BF16, name="w2_grouped", tag="grouped1", align_bytes=64)
         w2_scales = keep.tile([P, N], U8, name="w2_scales", align_bytes=64)
         nc.gpsimd.tensor_scalar(
-            w2_grouped[:].rearrange("p (n j) -> p n j", j=PACK),
-            w2_raw.rearrange("p j n -> p n j"),
+            w2_grouped[:].rearrange("p (n t) -> p n t", t=PACK),
+            w2_raw.rearrange("p t n -> p n t"),
             1.0,
             0.0,
             mybir.AluOpType.mult,
@@ -154,80 +170,72 @@ def tile_picked_phpool_gelu_p_kernel(tc, x_words, x_scales, w1, w2, offs, out):
 
         largers = [keep.tile([P, PACK, CHUNK], F32, name="larger%d" % c) for c in range(CHUNKS)]
 
-        def larger_of(c, t, shared):
+        def larger_shared(c, t):
             reads = banks[c][t][:].rearrange("p (r v) -> p r v", r=2)
-            if shared:
-                first_read = keep.tile([P, CHUNK], F32, name="first_read%d%d" % (c, t), tag="first_read%d%d" % (c, t), align_bytes=64)
-                nc.scalar.copy(first_read[:], reads[:, 0, :])
-                nc.vector.tensor_tensor(largers[c][:, t, :], first_read[:], reads[:, 1, :], MAX)
-            else:
-                nc.vector.tensor_reduce(largers[c][:, t, :], reads.rearrange("p r v -> p v r"), mybir.AxisListType.X, MAX)
+            one_read = keep.tile([P, CHUNK], F32, name="one_read%d%d" % (c, t), tag="one_read%d%d" % (c, t), align_bytes=64)
+            nc.scalar.copy(one_read[:], reads[:, 0, :])
+            nc.vector.tensor_tensor(largers[c][:, t, :], one_read[:], reads[:, 1, :], MAX)
 
-        pieces = [(c, v0, P) for c in range(CHUNKS) for v0 in range(0, CHUNK, P)]
-        z_grouped = [keep.tile([P, PACK * n], BF16, name="z_grouped%d" % i, align_bytes=64) for i, (c, v0, n) in enumerate(pieces)]
+        def larger_on_vector(c, t):
+            reads = banks[c][t][:].rearrange("p (r v) -> p v r", r=2)
+            nc.vector.tensor_reduce(largers[c][:, t, :], reads, mybir.AxisListType.X, MAX)
+
+        pieces = [(c, v0) for c in range(CHUNKS) for v0 in range(0, CHUNK, PIECE)]
+        z_grouped = [keep.tile([P, PACK * PIECE], BF16, name="z_grouped%d" % i, align_bytes=64) for i in range(len(pieces))]
 
         def gelu(i):
-            c, v0, n = pieces[i]
+            c, v0 = pieces[i]
             nc.scalar.activation(
-                z_grouped[i][:].rearrange("p (c i t) -> p c t i", i=4, t=PACK),
-                largers[c][:, :, v0 : v0 + n].rearrange("p t (c i) -> p c t i", i=4),
+                z_grouped[i][:].rearrange("p (l u t) -> p l t u", u=LINE, t=PACK),
+                largers[c][:, :, v0 : v0 + PIECE].rearrange("p t (l u) -> p l t u", u=LINE),
                 GELU,
+                bias=no_bias[:],
             )
 
-        out_rows = out.rearrange("(h p) v -> p h v", p=P)
-
-        def second_product(i, tags):
-            c, v0, n = pieces[i]
-            z_codes = all_codes[:, c * CHUNK + v0 : c * CHUNK + v0 + n]
-            z_scales = keep.tile([P, n], U8, name="z_scales%d" % i, align_bytes=64)
-            nc.vector.quantize_mx(out=z_codes.bitcast(FP8X4), scales=z_scales[:], in_=z_grouped[i][:])
-            if len(tags) == 1:
-                both = psum.tile([P, 2, n], F32, name="acc%d" % i, tag=tags[0])
-                accs = [both[:, h, :] for h in range(2)]
-            else:
-                both = None
-                accs = [psum.tile([P, n], F32, name="acc%d_%d" % (i, h), tag=tags[h])[:] for h in range(2)]
+        def second_product(i, accs):
+            codes = z_codes[:, PIECE * i : PIECE * (i + 1)].bitcast(FP8X4)
+            z_scales = keep.tile([P, PIECE], U8, name="z_scales%d" % i, align_bytes=64)
+            nc.vector.quantize_mx(out=codes, scales=z_scales[:], in_=z_grouped[i][:])
             for h in range(2):
                 nc.tensor.matmul_mx(
                     out=accs[h],
                     lhsT=w2_codes[:, P * h : P * (h + 1)].bitcast(FP8X4),
                     lhsT_scale=w2_scales[:, P * h : P * (h + 1)],
-                    rhs=z_codes.bitcast(FP8X4),
+                    rhs=codes,
                     rhs_scale=z_scales[:],
                     start=True,
                     stop=True,
                 )
-            return both, accs
-
-        def store(i, copy, both, accs):
-            c, v0, n = pieces[i]
-            cols = slice(c * CHUNK + v0, c * CHUNK + v0 + n)
-            result = keep.tile([P, 2, n], F32, name="result%d" % i)
-            if both is not None:
-                copy(result[:], both[:])
-            else:
-                nc.vector.tensor_copy(result[:, 0, :], accs[0])
-                nc.scalar.copy(result[:, 1, :], accs[1])
-            nc.sync.dma_start(out_rows[:, :, cols], result[:])
 
         for t in range(PACK):
-            larger_of(0, t, True)
-        larger_of(1, 0, True)
-        larger_of(1, 1, True)
-        larger_of(1, 2, True)
-        larger_of(1, 3, False)
+            larger_shared(0, t)
+        larger_shared(1, 0)
+        larger_shared(1, 1)
         gelu(0)
-        w2_codes = keep.tile([P, N], U32, name="w2_codes", tag="first_read03", align_bytes=64)
+        larger_shared(1, 2)
+        larger_on_vector(1, 3)
+        w2_codes = keep.tile([P, N], U32, name="w2_codes", tag="one_read03", align_bytes=64)
         nc.vector.quantize_mx(out=w2_codes[:].bitcast(FP8X4), scales=w2_scales[:], in_=w2_grouped[:])
-        all_codes = keep.tile([P, V], U32, name="all_codes", tag="grouped1", align_bytes=64)
-        results = [second_product(0, ["bank0"])]
-        gelu(1)
-        results.append(second_product(1, ["bank1"]))
-        gelu(2)
-        results.append(second_product(2, ["bank2"]))
-        gelu(3)
-        results.append(second_product(3, ["bank3", "bank4"]))
-        store(0, nc.scalar.copy, *results[0])
-        store(1, nc.scalar.copy, *results[1])
-        store(2, nc.vector.tensor_copy, *results[2])
-        store(3, None, *results[3])
+        z_codes = keep.tile([P, V], U32, name="z_codes", tag="grouped1", align_bytes=64)
+
+        last = len(pieces) - 1
+        paired = []
+        for i in range(last):
+            if i > 0:
+                gelu(i)
+            paired.append(psum.tile([P, 2, PIECE], F32, name="acc%d" % i, tag="bank%d" % i))
+            second_product(i, [paired[i][:, h, :] for h in range(2)])
+        gelu(last)
+        apart = [psum.tile([P, PIECE], F32, name="acc%d_%d" % (last, h), tag="bank%d" % (last + h))[:] for h in range(2)]
+        second_product(last, apart)
+
+        out_rows = out.rearrange("(h p) v -> p h v", p=P)
+        for i, copy in enumerate((nc.scalar.copy, nc.scalar.copy, nc.vector.tensor_copy)):
+            result = keep.tile([P, 2, PIECE], F32, name="result%d" % i)
+            copy(result[:], paired[i][:])
+            nc.sync.dma_start(out_rows[:, :, PIECE * i : PIECE * (i + 1)], result[:])
+        result = keep.tile([P, 2, PIECE], F32, name="result%d" % last)
+        nc.vector.tensor_copy(result[:, 0, :], apart[0])
+        nc.sync.dma_start(out_rows[:, 0, PIECE * last : V], result[:, 0, :])
+        nc.scalar.copy(result[:, 1, :], apart[1])
+        nc.scalar.dma_start(out_rows[:, 1, PIECE * last : V], result[:, 1, :])

@@ -57,9 +57,9 @@ def tile_picked_phpool_gelu_p_kernel(tc, x_words, x_scales, w1, w2, offs, out):
         no_bias = keep.tile([P, 1], F32, name="no_bias")
         nc.scalar.activation(no_bias[:], zero[:], GELU)
 
+        nc.sync.dma_start(word_table[0][:], x_rows[0])
         load_w1(0, 1)
-        for z in range(PASSES):
-            nc.sync.dma_start(word_table[z][:], x_rows[z])
+        nc.sync.dma_start(word_table[1][:], x_rows[1])
 
         def gather(picked, table):
             for first, count, at in ((CHUNK, 2 * CHUNK, CHUNK), (0, CHUNK, 3 * CHUNK), (3 * CHUNK, CHUNK, 0)):
@@ -122,25 +122,25 @@ def tile_picked_phpool_gelu_p_kernel(tc, x_words, x_scales, w1, w2, offs, out):
         all_banks = [(c, t) for c in range(CHUNKS) for t in range(PACK)]
         early_banks, late_banks = all_banks[:EARLY_BANKS], all_banks[EARLY_BANKS:]
 
-        for h in range(2):
-            deal(0, h, 0, PACK, nc.scalar.copy)
-        quantize_w1(0, 0, PACK)
-        first_words = keep.tile([P, S], U32, name="first_words", tag="grouped0", align_bytes=64)
+        first_words = keep.tile([P, S], U32, name="first_words", align_bytes=64)
         gather(first_words, word_table[0][:].bitcast(U32))
         for scratch in scratch_banks:
             nc.tensor.matmul_mx(
                 out=scratch[:],
-                lhsT=w1_codes[0][:, 0:P].bitcast(FP8X4),
-                lhsT_scale=w1_scales[0][:, 0:P],
+                lhsT=first_words[:, 3 * CHUNK : 3 * CHUNK + P].bitcast(FP8X4),
+                lhsT_scale=picked_scales[:, 3 * CHUNK : 3 * CHUNK + P],
                 rhs=first_words[:, CHUNK : 3 * CHUNK].bitcast(FP8X4),
-                rhs_scale=w1_scales[0][:],
+                rhs_scale=picked_scales[:, CHUNK : 3 * CHUNK],
                 start=True,
                 stop=True,
             )
+        for h in range(2):
+            deal(0, h, 0, PACK, nc.scalar.copy)
+        quantize_w1(0, 0, PACK)
         picked_words = [first_words]
         for c, t in early_banks:
             one_pass(0, c, t, True)
-        last_words = keep.tile([P, S], U32, name="last_words", align_bytes=64)
+        last_words = keep.tile([P, S], U32, name="last_words", tag="grouped0", align_bytes=64)
         gather(last_words, word_table[1][:].bitcast(U32))
 
         deal(1, 0, 0, PACK, nc.scalar.copy)

@@ -25,7 +25,9 @@ CHUNKS = V // CHUNK
 PIECE = 128
 HALF = H // 2
 GROUPS = HALF // (PACK * LINE)
+ROW_TILES = N // P
 QUADRANT = 32
+QUADRANT_ORDER = (0, 2, 1, 3)
 WARM_UPS = 2
 EARLY_BANKS = CHUNKS * PACK - 1
 
@@ -68,7 +70,7 @@ def tile_picked_phpool_gelu_p_kernel(tc, x_words, x_scales, w1, w2, offs, out):
 
         picked_scales = keep.tile([P, S], U8, name="picked_scales", align_bytes=64)
         gather(picked_scales, scale_table[:])
-        for q in range(P // QUADRANT):
+        for q in QUADRANT_ORDER:
             nc.sync.dma_start(
                 planes[QUADRANT * q : QUADRANT * q + 4].bitcast(I32),
                 picked_scales[QUADRANT * q : QUADRANT * (q + 1) : 4, :].bitcast(I32),
@@ -88,8 +90,8 @@ def tile_picked_phpool_gelu_p_kernel(tc, x_words, x_scales, w1, w2, offs, out):
             keep.tile([P, PACK * H], BF16, name="w1_grouped%d" % z, tag="grouped%d" % z, align_bytes=64) for z in range(PASSES)
         ]
 
-        def deal(z, h, t0, t1, copy):
-            copy(
+        def deal(z, h, t0, t1):
+            nc.scalar.copy(
                 w1_grouped[z][:].rearrange("p (t g u j) -> p g t j u", t=PACK, u=LINE, j=PACK)[:, GROUPS * h : GROUPS * (h + 1), t0:t1],
                 w1_raw[z][h].rearrange("p j (g t u) -> p g t j u", t=PACK, u=LINE)[:, :, t0:t1],
             )
@@ -135,7 +137,7 @@ def tile_picked_phpool_gelu_p_kernel(tc, x_words, x_scales, w1, w2, offs, out):
                 stop=True,
             )
         for h in range(2):
-            deal(0, h, 0, PACK, nc.scalar.copy)
+            deal(0, h, 0, PACK)
         quantize_w1(0, 0, PACK)
         picked_words = [first_words]
         for c, t in early_banks:
@@ -143,12 +145,9 @@ def tile_picked_phpool_gelu_p_kernel(tc, x_words, x_scales, w1, w2, offs, out):
         last_words = keep.tile([P, S], U32, name="last_words", tag="grouped0", align_bytes=64)
         gather(last_words, word_table[1][:].bitcast(U32))
 
-        deal(1, 0, 0, PACK, nc.scalar.copy)
-        for t in range(PACK - 1):
-            deal(1, 1, t, t + 1, nc.scalar.copy)
-        quantize_w1(1, 0, 1)
-        deal(1, 1, PACK - 1, PACK, nc.vector.tensor_copy)
-        for t in range(1, PACK):
+        deal(1, 0, 0, PACK)
+        for t in range(PACK):
+            deal(1, 1, t, t + 1)
             quantize_w1(1, t, t + 1)
         picked_words.append(last_words)
         for c, t in early_banks:
@@ -196,11 +195,11 @@ def tile_picked_phpool_gelu_p_kernel(tc, x_words, x_scales, w1, w2, offs, out):
             codes = z_codes[:, PIECE * i : PIECE * (i + 1)].bitcast(FP8X4)
             z_scales = keep.tile([P, PIECE], U8, name="z_scales%d" % i, align_bytes=64)
             nc.vector.quantize_mx(out=codes, scales=z_scales[:], in_=z_grouped[i][:])
-            for h in range(2):
+            for m in range(ROW_TILES):
                 nc.tensor.matmul_mx(
-                    out=accs[h],
-                    lhsT=w2_codes[:, P * h : P * (h + 1)].bitcast(FP8X4),
-                    lhsT_scale=w2_scales[:, P * h : P * (h + 1)],
+                    out=accs[m],
+                    lhsT=w2_codes[:, P * m : P * (m + 1)].bitcast(FP8X4),
+                    lhsT_scale=w2_scales[:, P * m : P * (m + 1)],
                     rhs=codes,
                     rhs_scale=z_scales[:],
                     start=True,
@@ -223,18 +222,19 @@ def tile_picked_phpool_gelu_p_kernel(tc, x_words, x_scales, w1, w2, offs, out):
         for i in range(last):
             if i > 0:
                 gelu(i)
-            paired.append(psum.tile([P, 2, PIECE], F32, name="acc%d" % i, tag="bank%d" % i))
-            second_product(i, [paired[i][:, h, :] for h in range(2)])
+            paired.append(psum.tile([P, ROW_TILES, PIECE], F32, name="acc%d" % i, tag="bank%d" % i))
+            second_product(i, [paired[i][:, m, :] for m in range(ROW_TILES)])
         gelu(last)
-        apart = [psum.tile([P, PIECE], F32, name="acc%d_%d" % (last, h), tag="bank%d" % (last + h))[:] for h in range(2)]
+        apart = [psum.tile([P, PIECE], F32, name="acc%d_%d" % (last, m), tag="bank%d" % (last + m))[:] for m in range(ROW_TILES)]
         second_product(last, apart)
 
-        out_rows = out.rearrange("(h p) v -> p h v", p=P)
-        for i, copy in enumerate((nc.scalar.copy, nc.scalar.copy, nc.vector.tensor_copy)):
-            result = keep.tile([P, 2, PIECE], F32, name="result%d" % i)
+        out_rows = out.rearrange("(m p) v -> p m v", p=P)
+        by_scalar, by_vector = (nc.scalar.copy, nc.scalar.dma_start), (nc.vector.tensor_copy, nc.sync.dma_start)
+        for i, (copy, store) in enumerate((by_scalar, by_scalar, by_vector)):
+            result = keep.tile([P, ROW_TILES, PIECE], F32, name="result%d" % i)
             copy(result[:], paired[i][:])
-            nc.sync.dma_start(out_rows[:, :, PIECE * i : PIECE * (i + 1)], result[:])
-        result = keep.tile([P, 2, PIECE], F32, name="result%d" % last)
+            store(out_rows[:, :, PIECE * i : PIECE * (i + 1)], result[:])
+        result = keep.tile([P, ROW_TILES, PIECE], F32, name="result%d" % last)
         nc.vector.tensor_copy(result[:, 0, :], apart[0])
         nc.sync.dma_start(out_rows[:, 0, PIECE * last : V], result[:, 0, :])
         nc.scalar.copy(result[:, 1, :], apart[1])

@@ -157,15 +157,15 @@ def tile_picked_phpool_gelu_p_kernel(tc, x_words, x_scales, w1, w2, offs, out):
             one_pass(0, c, t, False)
 
         w2_grouped = keep.tile([P, PACK * N], BF16, name="w2_grouped", tag="grouped1", align_bytes=64)
-        w2_scales = keep.tile([P, N], U8, name="w2_scales", align_bytes=64)
-        nc.gpsimd.tensor_scalar(
-            w2_grouped[:].rearrange("p (n t) -> p n t", t=PACK),
-            w2_raw.rearrange("p t n -> p n t"),
-            1.0,
-            0.0,
-            mybir.AluOpType.mult,
-            mybir.AluOpType.add,
-        )
+        for m in range(ROW_TILES):
+            nc.gpsimd.tensor_scalar(
+                w2_grouped[:].rearrange("p (n t) -> p n t", t=PACK)[:, P * m : P * (m + 1)],
+                w2_raw.rearrange("p t n -> p n t")[:, P * m : P * (m + 1)],
+                1.0,
+                0.0,
+                mybir.AluOpType.mult,
+                mybir.AluOpType.add,
+            )
 
         largers = [keep.tile([P, PACK, CHUNK], F32, name="larger%d" % c) for c in range(CHUNKS)]
 
@@ -175,9 +175,9 @@ def tile_picked_phpool_gelu_p_kernel(tc, x_words, x_scales, w1, w2, offs, out):
             nc.scalar.copy(one_read[:], reads[:, 0, :])
             nc.vector.tensor_tensor(largers[c][:, t, :], one_read[:], reads[:, 1, :], MAX)
 
-        def larger_on_vector(c, t):
-            reads = banks[c][t][:].rearrange("p (r v) -> p v r", r=2)
-            nc.vector.tensor_reduce(largers[c][:, t, :], reads, mybir.AxisListType.X, MAX)
+        def larger_on_vector(c, t, v0):
+            reads = banks[c][t][:].rearrange("p (r v) -> p v r", r=2)[:, v0 : v0 + PIECE]
+            nc.vector.tensor_reduce(largers[c][:, t, v0 : v0 + PIECE], reads, mybir.AxisListType.X, MAX)
 
         pieces = [(c, v0) for c in range(CHUNKS) for v0 in range(0, CHUNK, PIECE)]
         z_grouped = [keep.tile([P, PACK * PIECE], BF16, name="z_grouped%d" % i, align_bytes=64) for i in range(len(pieces))]
@@ -191,42 +191,56 @@ def tile_picked_phpool_gelu_p_kernel(tc, x_words, x_scales, w1, w2, offs, out):
                 bias=no_bias[:],
             )
 
-        def second_product(i, accs):
-            codes = z_codes[:, PIECE * i : PIECE * (i + 1)].bitcast(FP8X4)
-            z_scales = keep.tile([P, PIECE], U8, name="z_scales%d" % i, align_bytes=64)
-            nc.vector.quantize_mx(out=codes, scales=z_scales[:], in_=z_grouped[i][:])
-            for m in range(ROW_TILES):
-                nc.tensor.matmul_mx(
-                    out=accs[m],
-                    lhsT=w2_codes[:, P * m : P * (m + 1)].bitcast(FP8X4),
-                    lhsT_scale=w2_scales[:, P * m : P * (m + 1)],
-                    rhs=codes,
-                    rhs_scale=z_scales[:],
-                    start=True,
-                    stop=True,
-                )
+        z_codes = [keep.tile([P, PIECE], U32, name="z_codes%d" % i, align_bytes=64) for i in range(len(pieces))]
+        z_scales = [keep.tile([P, PIECE], U8, name="z_scales%d" % i, align_bytes=64) for i in range(len(pieces))]
+        w2_codes, w2_scales = {}, {}
+
+        def quantize_w2(m, behind):
+            w2_codes[m] = keep.tile([P, P], U32, name="w2_codes%d" % m, tag=behind, align_bytes=64)
+            w2_scales[m] = keep.tile([P, P], U8, name="w2_scales%d" % m, align_bytes=64)
+            nc.vector.quantize_mx(
+                out=w2_codes[m][:].bitcast(FP8X4), scales=w2_scales[m][:], in_=w2_grouped[:, PACK * P * m : PACK * P * (m + 1)]
+            )
+
+        def quantize_z(i):
+            nc.vector.quantize_mx(out=z_codes[i][:].bitcast(FP8X4), scales=z_scales[i][:], in_=z_grouped[i][:])
+
+        def product(i, m, acc):
+            nc.tensor.matmul_mx(
+                out=acc,
+                lhsT=w2_codes[m][:].bitcast(FP8X4),
+                lhsT_scale=w2_scales[m][:],
+                rhs=z_codes[i][:].bitcast(FP8X4),
+                rhs_scale=z_scales[i][:],
+                start=True,
+                stop=True,
+            )
 
         for t in range(PACK):
             larger_shared(0, t)
         larger_shared(1, 0)
         larger_shared(1, 1)
-        gelu(0)
         larger_shared(1, 2)
-        larger_on_vector(1, 3)
-        w2_codes = keep.tile([P, N], U32, name="w2_codes", tag="one_read03", align_bytes=64)
-        nc.vector.quantize_mx(out=w2_codes[:].bitcast(FP8X4), scales=w2_scales[:], in_=w2_grouped[:])
-        z_codes = keep.tile([P, V], U32, name="z_codes", tag="grouped1", align_bytes=64)
-
+        for v0 in range(0, CHUNK, PIECE):
+            larger_on_vector(1, 3, v0)
+        gelu(0)
         last = len(pieces) - 1
-        paired = []
-        for i in range(last):
-            if i > 0:
-                gelu(i)
-            paired.append(psum.tile([P, ROW_TILES, PIECE], F32, name="acc%d" % i, tag="bank%d" % i))
-            second_product(i, [paired[i][:, m, :] for m in range(ROW_TILES)])
-        gelu(last)
+        paired = [psum.tile([P, ROW_TILES, PIECE], F32, name="acc%d" % i, tag="bank%d" % i) for i in range(last)]
         apart = [psum.tile([P, PIECE], F32, name="acc%d_%d" % (last, m), tag="bank%d" % (last + m))[:] for m in range(ROW_TILES)]
-        second_product(last, apart)
+        quantize_w2(0, "one_read03")
+        quantize_z(0)
+        product(0, 0, paired[0][:, 0, :])
+        gelu(1)
+        quantize_z(1)
+        product(1, 0, paired[1][:, 0, :])
+        quantize_w2(1, "one_read12")
+        product(0, 1, paired[0][:, 1, :])
+        product(1, 1, paired[1][:, 1, :])
+        for i in (2, last):
+            gelu(i)
+            quantize_z(i)
+            for m in range(ROW_TILES):
+                product(i, m, paired[i][:, m, :] if i < last else apart[m])
 
         out_rows = out.rearrange("(m p) v -> p m v", p=P)
         by_scalar, by_vector = (nc.scalar.copy, nc.scalar.dma_start), (nc.vector.tensor_copy, nc.sync.dma_start)

@@ -41,12 +41,9 @@ def tile_picked_phpool_gelu_p_kernel(tc, x_words, x_scales, w1, w2, offs, out):
         w1_rows = [w1[P * PACK * z : P * PACK * (z + 1), :].rearrange("(p j) c -> p j c", j=PACK) for z in range(PASSES)]
         x_rows = [x_words[z].rearrange("p n j -> p (n j)").bitcast(I32) for z in range(PASSES)]
         word_table = [keep.tile([P, T], I32, name="word_table%d" % z) for z in range(PASSES)]
-        w1_raw = [[keep.tile([P, PACK, HALF], F32, name="w1_raw0%d" % h)[:] for h in range(2)]]
+        w1_pairs = [keep.tile([P, 2, H], F32, name="w1_pair%d" % h) for h in range(2)]
 
-        def load_w1(z, h):
-            nc.sync.dma_start(w1_raw[z][h], w1_rows[z][:, :, HALF * h : HALF * (h + 1)])
-
-        load_w1(0, 0)
+        nc.sync.dma_start(w1_pairs[0][:], w1_rows[0][:, 0:2])
         offsets = keep.tile([P, S // LIST_ROWS], U16, name="offsets")
         nc.sync.dma_start(offsets[:], offs)
         scale_table = keep.tile([P, T], U8, name="scale_table", tag="scale_table", align_bytes=64)
@@ -60,7 +57,7 @@ def tile_picked_phpool_gelu_p_kernel(tc, x_words, x_scales, w1, w2, offs, out):
         nc.scalar.activation(no_bias[:], zero[:], GELU)
 
         nc.sync.dma_start(word_table[0][:], x_rows[0])
-        load_w1(0, 1)
+        nc.sync.dma_start(w1_pairs[1][:], w1_rows[0][:, 2:4])
         nc.sync.dma_start(word_table[1][:], x_rows[1])
 
         def gather(picked, table):
@@ -76,9 +73,9 @@ def tile_picked_phpool_gelu_p_kernel(tc, x_words, x_scales, w1, w2, offs, out):
                 picked_scales[QUADRANT * q : QUADRANT * (q + 1) : 4, :].bitcast(I32),
             )
         late = keep.tile([P, 3, PACK, HALF], F32, name="late", tag="scale_table", align_bytes=64)
-        w1_raw.append([late[:, h] for h in range(2)])
-        load_w1(1, 0)
-        load_w1(1, 1)
+        w1_halves = [late[:, h] for h in range(2)]
+        for h in range(2):
+            nc.sync.dma_start(w1_halves[h], w1_rows[1][:, :, HALF * h : HALF * (h + 1)])
         w2_raw = late[:, 2]
         w2_rows = w2.rearrange("(g t u) n -> t g u n", t=PACK, u=LINE)
         for t in range(PACK):
@@ -90,10 +87,15 @@ def tile_picked_phpool_gelu_p_kernel(tc, x_words, x_scales, w1, w2, offs, out):
             keep.tile([P, PACK * H], BF16, name="w1_grouped%d" % z, tag="grouped%d" % z, align_bytes=64) for z in range(PASSES)
         ]
 
-        def deal(z, h, t0, t1):
+        dealt = [grouped[:].rearrange("p (t g u j) -> p g t j u", t=PACK, u=LINE, j=PACK) for grouped in w1_grouped]
+
+        def deal_pair(h):
+            nc.scalar.copy(dealt[0][:, :, :, 2 * h : 2 * h + 2], w1_pairs[h][:].rearrange("p j (g t u) -> p g t j u", t=PACK, u=LINE))
+
+        def deal_half(h, t0, t1):
             nc.scalar.copy(
-                w1_grouped[z][:].rearrange("p (t g u j) -> p g t j u", t=PACK, u=LINE, j=PACK)[:, GROUPS * h : GROUPS * (h + 1), t0:t1],
-                w1_raw[z][h].rearrange("p j (g t u) -> p g t j u", t=PACK, u=LINE)[:, :, t0:t1],
+                dealt[1][:, GROUPS * h : GROUPS * (h + 1), t0:t1],
+                w1_halves[h].rearrange("p j (g t u) -> p g t j u", t=PACK, u=LINE)[:, :, t0:t1],
             )
 
         def quantize_w1(z, t0, t1):
@@ -137,7 +139,7 @@ def tile_picked_phpool_gelu_p_kernel(tc, x_words, x_scales, w1, w2, offs, out):
                 stop=True,
             )
         for h in range(2):
-            deal(0, h, 0, PACK)
+            deal_pair(h)
         quantize_w1(0, 0, PACK)
         picked_words = [first_words]
         for c, t in early_banks:
@@ -145,9 +147,9 @@ def tile_picked_phpool_gelu_p_kernel(tc, x_words, x_scales, w1, w2, offs, out):
         last_words = keep.tile([P, S], U32, name="last_words", tag="grouped0", align_bytes=64)
         gather(last_words, word_table[1][:].bitcast(U32))
 
-        deal(1, 0, 0, PACK)
+        deal_half(0, 0, PACK)
         for t in range(PACK):
-            deal(1, 1, t, t + 1)
+            deal_half(1, t, t + 1)
             quantize_w1(1, t, t + 1)
         picked_words.append(last_words)
         for c, t in early_banks:

@@ -169,7 +169,7 @@ def tile_picked_phpool_gelu_p_kernel(tc, x_words, x_scales, w1, w2, offs, out):
                 mybir.AluOpType.add,
             )
 
-        largers = [keep.tile([P, PACK, CHUNK], F32, name="larger%d" % c) for c in range(CHUNKS)]
+        largers = [keep.tile([P, PACK, CHUNK], F32, name="larger%d" % c, tag="larger%d" % c, align_bytes=64) for c in range(CHUNKS)]
 
         def larger_shared(c, t):
             reads = banks[c][t][:].rearrange("p (r v) -> p r v", r=2)
@@ -229,14 +229,14 @@ def tile_picked_phpool_gelu_p_kernel(tc, x_words, x_scales, w1, w2, offs, out):
         last = len(pieces) - 1
         paired = [psum.tile([P, ROW_TILES, PIECE], F32, name="acc%d" % i, tag="bank%d" % i) for i in range(last)]
         apart = [psum.tile([P, PIECE], F32, name="acc%d_%d" % (last, m), tag="bank%d" % (last + m))[:] for m in range(ROW_TILES)]
-        quantize_w2(0, "one_read03")
+        gelu(1)
+        quantize_w2(0, "one_read12")
         quantize_z(0)
         product(0, 0, paired[0][:, 0, :])
-        gelu(1)
+        quantize_w2(1, "larger0")
+        product(0, 1, paired[0][:, 1, :])
         quantize_z(1)
         product(1, 0, paired[1][:, 0, :])
-        quantize_w2(1, "one_read12")
-        product(0, 1, paired[0][:, 1, :])
         product(1, 1, paired[1][:, 1, :])
         for i in (2, last):
             gelu(i)

@@ -227,29 +227,32 @@ def tile_picked_phpool_gelu_p_kernel(tc, x_words, x_scales, w1, w2, offs, out):
             larger_on_vector(1, 3, v0)
         gelu(0)
         last = len(pieces) - 1
-        paired = [psum.tile([P, ROW_TILES, PIECE], F32, name="acc%d" % i, tag="bank%d" % i) for i in range(last)]
+        by_rows = [psum.tile([P, CHUNK], F32, name="rows%d" % m, tag="bank%d" % m) for m in range(ROW_TILES)]
+        paired = psum.tile([P, ROW_TILES, PIECE], F32, name="paired", tag="bank2")
         apart = [psum.tile([P, PIECE], F32, name="acc%d_%d" % (last, m), tag="bank%d" % (last + m))[:] for m in range(ROW_TILES)]
         gelu(1)
         quantize_w2(0, "one_read12")
         quantize_z(0)
-        product(0, 0, paired[0][:, 0, :])
-        quantize_w2(1, "larger0")
-        product(0, 1, paired[0][:, 1, :])
+        product(0, 0, by_rows[0][:, 0:PIECE])
         quantize_z(1)
-        product(1, 0, paired[1][:, 0, :])
-        product(1, 1, paired[1][:, 1, :])
+        product(1, 0, by_rows[0][:, PIECE:CHUNK])
+        quantize_w2(1, "larger0")
+        product(0, 1, by_rows[1][:, 0:PIECE])
+        product(1, 1, by_rows[1][:, PIECE:CHUNK])
         for i in (2, last):
             gelu(i)
             quantize_z(i)
             for m in range(ROW_TILES):
-                product(i, m, paired[i][:, m, :] if i < last else apart[m])
+                product(i, m, paired[:, m, :] if i < last else apart[m])
 
         out_rows = out.rearrange("(m p) v -> p m v", p=P)
-        by_scalar, by_vector = (nc.scalar.copy, nc.scalar.dma_start), (nc.vector.tensor_copy, nc.sync.dma_start)
-        for i, (copy, store) in enumerate((by_scalar, by_scalar, by_vector)):
-            result = keep.tile([P, ROW_TILES, PIECE], F32, name="result%d" % i)
-            copy(result[:], paired[i][:])
-            store(out_rows[:, :, PIECE * i : PIECE * (i + 1)], result[:])
+        for m in range(ROW_TILES):
+            result = keep.tile([P, CHUNK], F32, name="result%d" % m)
+            nc.scalar.copy(result[:], by_rows[m][:])
+            nc.scalar.dma_start(out_rows[:, m, 0:CHUNK], result[:])
+        result = keep.tile([P, ROW_TILES, PIECE], F32, name="result2")
+        nc.vector.tensor_copy(result[:], paired[:])
+        nc.sync.dma_start(out_rows[:, :, CHUNK : CHUNK + PIECE], result[:])
         result = keep.tile([P, ROW_TILES, PIECE], F32, name="result%d" % last)
         nc.vector.tensor_copy(result[:, 0, :], apart[0])
         nc.sync.dma_start(out_rows[:, 0, PIECE * last : V], result[:, 0, :])

@@ -89,8 +89,11 @@ def tile_picked_phpool_gelu_p_kernel(tc, x_words, x_scales, w1, w2, offs, out):
 
         dealt = [grouped[:].rearrange("p (t g u j) -> p g t j u", t=PACK, u=LINE, j=PACK) for grouped in w1_grouped]
 
-        def deal_pair(h):
-            nc.scalar.copy(dealt[0][:, :, :, 2 * h : 2 * h + 2], w1_pairs[h][:].rearrange("p j (g t u) -> p g t j u", t=PACK, u=LINE))
+        def deal_pair(h, t0, t1):
+            nc.scalar.copy(
+                dealt[0][:, :, t0:t1, 2 * h : 2 * h + 2],
+                w1_pairs[h][:].rearrange("p j (g t u) -> p g t j u", t=PACK, u=LINE)[:, :, t0:t1],
+            )
 
         def deal_half(h, t0, t1):
             nc.scalar.copy(
@@ -138,9 +141,10 @@ def tile_picked_phpool_gelu_p_kernel(tc, x_words, x_scales, w1, w2, offs, out):
                 start=True,
                 stop=True,
             )
-        for h in range(2):
-            deal_pair(h)
-        quantize_w1(0, 0, PACK)
+        deal_pair(0, 0, PACK)
+        for t in range(0, PACK, 2):
+            deal_pair(1, t, t + 2)
+            quantize_w1(0, t, t + 2)
         picked_words = [first_words]
         for c, t in early_banks:
             one_pass(0, c, t, True)

@@ -50,11 +50,11 @@ def tile_picked_phpool_gelu_p_kernel(tc, x_words, x_scales, w1, w2, offs, out):
         nc.vector.memset(scale_table[:].bitcast(I32), 0)
         nc.sync.dma_start(scale_table[0:P:4, :].bitcast(I32), x_scales.rearrange("z q c -> q z c").bitcast(I32))
         planes = keep.tile([P, PASSES, S], U8, name="planes", align_bytes=64)
-        nc.gpsimd.memset(planes[:].rearrange("p z s -> p (z s)").bitcast(I32), 0)
         zero = keep.tile([P, 1], F32, name="zero")
         nc.vector.memset(zero[:], 0.0)
         no_bias = keep.tile([P, 1], F32, name="no_bias")
         nc.scalar.activation(no_bias[:], zero[:], GELU)
+        nc.vector.memset(planes[:].rearrange("p z s -> p (z s)").bitcast(I32), 0)
 
         nc.sync.dma_start(word_table[0][:], x_rows[0])
         nc.sync.dma_start(w1_pairs[1][:], w1_rows[0][:, 2:4])

@@ -23,6 +23,7 @@ LIST_ROWS = 16
 CHUNK = 256
 CHUNKS = V // CHUNK
 PIECE = 128
+SHORT = PIECE // 2
 HALF = H // 2
 GROUPS = HALF // (PACK * LINE)
 ROW_TILES = N // P
@@ -185,20 +186,20 @@ def tile_picked_phpool_gelu_p_kernel(tc, x_words, x_scales, w1, w2, offs, out):
             reads = banks[c][t][:].rearrange("p (r v) -> p v r", r=2)[:, v0 : v0 + PIECE]
             nc.vector.tensor_reduce(largers[c][:, t, v0 : v0 + PIECE], reads, mybir.AxisListType.X, MAX)
 
-        pieces = [(c, v0) for c in range(CHUNKS) for v0 in range(0, CHUNK, PIECE)]
-        z_grouped = [keep.tile([P, PACK * PIECE], BF16, name="z_grouped%d" % i, align_bytes=64) for i in range(len(pieces))]
+        pieces = [(0, 0, PIECE), (0, PIECE, PIECE), (1, 0, PIECE), (1, PIECE, SHORT), (1, PIECE + SHORT, SHORT)]
+        z_grouped = [keep.tile([P, PACK * n], BF16, name="z_grouped%d" % i, align_bytes=64) for i, (c, v0, n) in enumerate(pieces)]
 
         def gelu(i):
-            c, v0 = pieces[i]
+            c, v0, n = pieces[i]
             nc.scalar.activation(
                 z_grouped[i][:].rearrange("p (l u t) -> p l t u", u=LINE, t=PACK),
-                largers[c][:, :, v0 : v0 + PIECE].rearrange("p t (l u) -> p l t u", u=LINE),
+                largers[c][:, :, v0 : v0 + n].rearrange("p t (l u) -> p l t u", u=LINE),
                 GELU,
                 bias=no_bias[:],
             )
 
-        z_codes = [keep.tile([P, PIECE], U32, name="z_codes%d" % i, align_bytes=64) for i in range(len(pieces))]
-        z_scales = [keep.tile([P, PIECE], U8, name="z_scales%d" % i, align_bytes=64) for i in range(len(pieces))]
+        z_codes = [keep.tile([P, n], U32, name="z_codes%d" % i, align_bytes=64) for i, (c, v0, n) in enumerate(pieces)]
+        z_scales = [keep.tile([P, n], U8, name="z_scales%d" % i, align_bytes=64) for i, (c, v0, n) in enumerate(pieces)]
         w2_codes, w2_scales = {}, {}
 
         def quantize_w2(m, behind):
@@ -233,7 +234,7 @@ def tile_picked_phpool_gelu_p_kernel(tc, x_words, x_scales, w1, w2, offs, out):
         last = len(pieces) - 1
         by_rows = [psum.tile([P, CHUNK], F32, name="rows%d" % m, tag="bank%d" % m) for m in range(ROW_TILES)]
         paired = psum.tile([P, ROW_TILES, PIECE], F32, name="paired", tag="bank2")
-        apart = [psum.tile([P, PIECE], F32, name="acc%d_%d" % (last, m), tag="bank%d" % (last + m))[:] for m in range(ROW_TILES)]
+        apart = [psum.tile([P, PIECE], F32, name="apart%d" % m, tag="bank%d" % (3 + m))[:] for m in range(ROW_TILES)]
         gelu(1)
         quantize_w2(0, "one_read12")
         quantize_z(0)
@@ -243,11 +244,12 @@ def tile_picked_phpool_gelu_p_kernel(tc, x_words, x_scales, w1, w2, offs, out):
         quantize_w2(1, "larger0")
         product(0, 1, by_rows[1][:, 0:PIECE])
         product(1, 1, by_rows[1][:, PIECE:CHUNK])
-        for i in (2, last):
+        for i in range(2, last + 1):
             gelu(i)
             quantize_z(i)
+            c, v0, n = pieces[i]
             for m in range(ROW_TILES):
-                product(i, m, paired[:, m, :] if i < last else apart[m])
+                product(i, m, paired[:, m, :] if n == PIECE else apart[m][:, v0 - PIECE : v0 - PIECE + n])
 
         out_rows = out.rearrange("(m p) v -> p m v", p=P)
         for m in range(ROW_TILES):
@@ -256,9 +258,9 @@ def tile_picked_phpool_gelu_p_kernel(tc, x_words, x_scales, w1, w2, offs, out):
             nc.scalar.dma_start(out_rows[:, m, 0:CHUNK], result[:])
         result = keep.tile([P, ROW_TILES, PIECE], F32, name="result2")
         nc.vector.tensor_copy(result[:], paired[:])
-        nc.sync.dma_start(out_rows[:, :, CHUNK : CHUNK + PIECE], result[:])
+        nc.sync.dma_start(out_rows[:, :, CHUNK : V - PIECE], result[:])
         result = keep.tile([P, ROW_TILES, PIECE], F32, name="result%d" % last)
         nc.vector.tensor_copy(result[:, 0, :], apart[0])
-        nc.sync.dma_start(out_rows[:, 0, PIECE * last : V], result[:, 0, :])
+        nc.sync.dma_start(out_rows[:, 0, V - PIECE : V], result[:, 0, :])
         nc.scalar.copy(result[:, 1, :], apart[1])
-        nc.scalar.dma_start(out_rows[:, 1, PIECE * last : V], result[:, 1, :])
+        nc.scalar.dma_start(out_rows[:, 1, V - PIECE : V], result[:, 1, :])

@@ -29,7 +29,7 @@ GROUPS = HALF // (PACK * LINE)
 ROW_TILES = N // P
 QUADRANT = 32
 QUADRANT_ORDER = (0, 2, 1, 3)
-WARM_UPS = 2
+WARM_UPS = (512, 256, 128)
 EARLY_BANKS = CHUNKS * PACK - 1
 
 
@@ -109,7 +109,7 @@ def tile_picked_phpool_gelu_p_kernel(tc, x_words, x_scales, w1, w2, offs, out):
                 in_=w1_grouped[z][:, H * t0 : H * t1],
             )
 
-        scratch_banks = [psum.tile([P, 2 * CHUNK], F32, name="scratch%d" % i, tag="bank%d" % i) for i in range(WARM_UPS)]
+        scratch_banks = [psum.tile([P, 2 * CHUNK], F32, name="scratch%d" % i, tag="bank%d" % i) for i in range(len(WARM_UPS))]
         banks = [
             [psum.tile([P, 2 * CHUNK], F32, name="y%d%d" % (c, t), tag="bank%d" % (PACK * c + t)) for t in range(PACK)]
             for c in range(CHUNKS)
@@ -132,13 +132,13 @@ def tile_picked_phpool_gelu_p_kernel(tc, x_words, x_scales, w1, w2, offs, out):
 
         first_words = keep.tile([P, S], U32, name="first_words", align_bytes=64)
         gather(first_words, word_table[0][:].bitcast(U32))
-        for scratch in scratch_banks:
+        for scratch, width in zip(scratch_banks, WARM_UPS):
             nc.tensor.matmul_mx(
-                out=scratch[:],
+                out=scratch[:, :width],
                 lhsT=first_words[:, 3 * CHUNK : 3 * CHUNK + P].bitcast(FP8X4),
                 lhsT_scale=picked_scales[:, 3 * CHUNK : 3 * CHUNK + P],
-                rhs=first_words[:, CHUNK : 3 * CHUNK].bitcast(FP8X4),
-                rhs_scale=picked_scales[:, CHUNK : 3 * CHUNK],
+                rhs=first_words[:, CHUNK : CHUNK + width].bitcast(FP8X4),
+                rhs_scale=picked_scales[:, CHUNK : CHUNK + width],
                 start=True,
                 stop=True,
             )
@@ -174,17 +174,23 @@ def tile_picked_phpool_gelu_p_kernel(tc, x_words, x_scales, w1, w2, offs, out):
                 mybir.AluOpType.add,
             )
 
-        largers = [keep.tile([P, PACK, CHUNK], F32, name="larger%d" % c, tag="larger%d" % c, align_bytes=64) for c in range(CHUNKS)]
+        largers = [keep.tile([P, CHUNK // LINE, PACK, LINE], F32, name="larger%d" % c, tag="larger%d" % c, align_bytes=64) for c in range(CHUNKS)]
 
         def larger_shared(c, t):
             reads = banks[c][t][:].rearrange("p (r v) -> p r v", r=2)
             one_read = keep.tile([P, CHUNK], F32, name="one_read%d%d" % (c, t), tag="one_read%d%d" % (c, t), align_bytes=64)
             nc.scalar.copy(one_read[:], reads[:, 0, :])
-            nc.vector.tensor_tensor(largers[c][:, t, :], one_read[:], reads[:, 1, :], MAX)
+            nc.vector.tensor_tensor(
+                largers[c][:, :, t],
+                one_read[:].rearrange("p (l u) -> p l u", u=LINE),
+                reads[:, 1, :].rearrange("p (l u) -> p l u", u=LINE),
+                MAX,
+            )
 
         def larger_on_vector(c, t, v0):
-            reads = banks[c][t][:].rearrange("p (r v) -> p v r", r=2)[:, v0 : v0 + PIECE]
-            nc.vector.tensor_reduce(largers[c][:, t, v0 : v0 + PIECE], reads, mybir.AxisListType.X, MAX)
+            lines = slice(v0 // LINE, (v0 + PIECE) // LINE)
+            reads = banks[c][t][:].rearrange("p (r l u) -> p l u r", r=2, u=LINE)[:, lines]
+            nc.vector.tensor_reduce(largers[c][:, lines, t], reads, mybir.AxisListType.X, MAX)
 
         pieces = [(0, 0, PIECE), (0, PIECE, PIECE), (1, 0, PIECE), (1, PIECE, SHORT), (1, PIECE + SHORT, SHORT)]
         z_grouped = [keep.tile([P, PACK * n], BF16, name="z_grouped%d" % i, align_bytes=64) for i, (c, v0, n) in enumerate(pieces)]
@@ -193,7 +199,7 @@ def tile_picked_phpool_gelu_p_kernel(tc, x_words, x_scales, w1, w2, offs, out):
             c, v0, n = pieces[i]
             nc.scalar.activation(
                 z_grouped[i][:].rearrange("p (l u t) -> p l t u", u=LINE, t=PACK),
-                largers[c][:, :, v0 : v0 + n].rearrange("p t (l u) -> p l t u", u=LINE),
+                largers[c][:, v0 // LINE : (v0 + n) // LINE],
                 GELU,
                 bias=no_bias[:],
             )

@@ -68,15 +68,20 @@ def tile_picked_phpool_gelu_p_kernel(tc, x_words, x_scales, w1, w2, offs, out):
 
         picked_scales = keep.tile([P, S], U8, name="picked_scales", align_bytes=64)
         gather(picked_scales, scale_table[:])
-        for q in QUADRANT_ORDER:
-            nc.sync.dma_start(
-                planes[QUADRANT * q : QUADRANT * q + 4].bitcast(I32),
-                picked_scales[QUADRANT * q : QUADRANT * (q + 1) : 4, :].bitcast(I32),
-            )
+
+        def move_scales(z):
+            for q in QUADRANT_ORDER:
+                first = QUADRANT * q + 4 * z
+                nc.sync.dma_start(
+                    planes[first : first + 4, z].bitcast(I32), picked_scales[first : QUADRANT * (q + 1) : 8, :].bitcast(I32)
+                )
+
+        move_scales(0)
         late = keep.tile([P, 3, PACK, HALF], F32, name="late", tag="scale_table", align_bytes=64)
         w1_halves = [late[:, h] for h in range(2)]
         for h in range(2):
             nc.sync.dma_start(w1_halves[h], w1_rows[1][:, :, HALF * h : HALF * (h + 1)])
+        move_scales(1)
         w2_raw = late[:, 2]
         w2_rows = w2.rearrange("(g t u) n -> t g u n", t=PACK, u=LINE)
         for t in range(PACK):
@@ -122,7 +127,7 @@ def tile_picked_phpool_gelu_p_kernel(tc, x_words, x_scales, w1, w2, offs, out):
                 lhsT=w1_codes[z][:, P * t : P * (t + 1)].bitcast(FP8X4),
                 lhsT_scale=w1_scales[z][:, P * t : P * (t + 1)],
                 rhs=picked_words[z][:, cols].bitcast(FP8X4),
-                rhs_scale=planes[:, z, cols],
+                rhs_scale=planes[4 * z :, z, cols],
                 start=start,
                 stop=not start,
             )

@@ -266,7 +266,7 @@ def tile_picked_phpool_gelu_p_kernel(tc, x_words, x_scales, w1, w2, offs, out):
         for m in range(ROW_TILES):
             result = keep.tile([P, CHUNK], F32, name="result%d" % m)
             nc.scalar.copy(result[:], by_rows[m][:])
-            nc.scalar.dma_start(out_rows[:, m, 0:CHUNK], result[:])
+            nc.sync.dma_start(out_rows[:, m, 0:CHUNK], result[:])
         result = keep.tile([P, ROW_TILES, PIECE], F32, name="result2")
         nc.vector.tensor_copy(result[:], paired[:])
         nc.sync.dma_start(out_rows[:, :, CHUNK : V - PIECE], result[:])

@@ -29,7 +29,8 @@ GROUPS = HALF // (PACK * LINE)
 ROW_TILES = N // P
 QUADRANT = 32
 QUADRANT_ORDER = (0, 2, 1, 3)
-WARM_UPS = (512, 256, 128)
+WARM_UPS = (512, 128)
+LATE_WARM_UP = 256
 EARLY_BANKS = CHUNKS * PACK - 1
 
 
@@ -137,7 +138,8 @@ def tile_picked_phpool_gelu_p_kernel(tc, x_words, x_scales, w1, w2, offs, out):
 
         first_words = keep.tile([P, S], U32, name="first_words", align_bytes=64)
         gather(first_words, word_table[0][:].bitcast(U32))
-        for scratch, width in zip(scratch_banks, WARM_UPS):
+
+        def warm_up(scratch, width):
             nc.tensor.matmul_mx(
                 out=scratch[:, :width],
                 lhsT=first_words[:, 3 * CHUNK : 3 * CHUNK + P].bitcast(FP8X4),
@@ -147,6 +149,9 @@ def tile_picked_phpool_gelu_p_kernel(tc, x_words, x_scales, w1, w2, offs, out):
                 start=True,
                 stop=True,
             )
+
+        for scratch, width in zip(scratch_banks, WARM_UPS):
+            warm_up(scratch, width)
         deal_pair(0, 0, PACK)
         for t in range(0, PACK, 2):
             deal_pair(1, t, t + 2)
@@ -239,6 +244,7 @@ def tile_picked_phpool_gelu_p_kernel(tc, x_words, x_scales, w1, w2, offs, out):
         larger_shared(1, 0)
         larger_shared(1, 1)
         larger_shared(1, 2)
+        warm_up(psum.tile([P, LATE_WARM_UP], F32, name="late_scratch", tag="bank6"), LATE_WARM_UP)
         for v0 in range(0, CHUNK, PIECE):
             larger_on_vector(1, 3, v0)
         gelu(0)

@@ -27,6 +27,7 @@ SHORT = PIECE // 2
 HALF = H // 2
 GROUPS = HALF // (PACK * LINE)
 ROW_TILES = N // P
+BURST = 256
 QUADRANT = 32
 QUADRANT_ORDER = (0, 2, 1, 3)
 WARM_UPS = (512, 128)
@@ -42,16 +43,16 @@ def tile_picked_phpool_gelu_p_kernel(tc, x_words, x_scales, w1, w2, offs, out):
 
         w1_rows = [w1[P * PACK * z : P * PACK * (z + 1), :].rearrange("(p j) c -> p j c", j=PACK) for z in range(PASSES)]
         x_rows = [x_words[z].rearrange("p n j -> p (n j)").bitcast(I32) for z in range(PASSES)]
-        word_table = [keep.tile([P, T], I32, name="word_table%d" % z) for z in range(PASSES)]
-        w1_pairs = [keep.tile([P, 2, H], F32, name="w1_pair%d" % h) for h in range(2)]
+        word_table = [keep.tile([P, T], I32, name="word_table%d" % z, align_bytes=BURST) for z in range(PASSES)]
+        w1_pairs = [keep.tile([P, 2, H], F32, name="w1_pair%d" % h, align_bytes=BURST) for h in range(2)]
 
         nc.sync.dma_start(w1_pairs[0][:], w1_rows[0][:, 0:2])
         offsets = keep.tile([P, S // LIST_ROWS], U16, name="offsets")
         nc.sync.dma_start(offsets[:], offs)
-        scale_table = keep.tile([P, T], U8, name="scale_table", tag="scale_table", align_bytes=64)
+        scale_table = keep.tile([P, T], U8, name="scale_table", tag="scale_table", align_bytes=BURST)
         nc.vector.memset(scale_table[:].bitcast(I32), 0)
         nc.sync.dma_start(scale_table[0:P:4, :].bitcast(I32), x_scales.rearrange("z q c -> q z c").bitcast(I32))
-        planes = keep.tile([P, PASSES, S], U8, name="planes", align_bytes=64)
+        planes = keep.tile([P, PASSES, S], U8, name="planes", align_bytes=BURST)
         zero = keep.tile([P, 1], F32, name="zero")
         nc.vector.memset(zero[:], 0.0)
         no_bias = keep.tile([P, 1], F32, name="no_bias")
@@ -67,7 +68,7 @@ def tile_picked_phpool_gelu_p_kernel(tc, x_words, x_scales, w1, w2, offs, out):
                 entries = offsets[:, first // LIST_ROWS : (first + count) // LIST_ROWS]
                 nc.vector.tensor_copy(picked[:, at : at + count], table.indirect(entries))
 
-        picked_scales = keep.tile([P, S], U8, name="picked_scales", align_bytes=64)
+        picked_scales = keep.tile([P, S], U8, name="picked_scales", align_bytes=BURST)
         gather(picked_scales, scale_table[:])
 
         def move_scales(z):
@@ -78,7 +79,7 @@ def tile_picked_phpool_gelu_p_kernel(tc, x_words, x_scales, w1, w2, offs, out):
                 )
 
         move_scales(0)
-        late = keep.tile([P, 3, PACK, HALF], F32, name="late", tag="scale_table", align_bytes=64)
+        late = keep.tile([P, 3, PACK, HALF], F32, name="late", tag="scale_table", align_bytes=BURST)
         w1_halves = [late[:, h] for h in range(2)]
         for h in range(2):
             nc.sync.dma_start(w1_halves[h], w1_rows[1][:, :, HALF * h : HALF * (h + 1)])
@@ -270,13 +271,13 @@ def tile_picked_phpool_gelu_p_kernel(tc, x_words, x_scales, w1, w2, offs, out):
 
         out_rows = out.rearrange("(m p) v -> p m v", p=P)
         for m in range(ROW_TILES):
-            result = keep.tile([P, CHUNK], F32, name="result%d" % m)
+            result = keep.tile([P, CHUNK], F32, name="result%d" % m, align_bytes=BURST)
             nc.scalar.copy(result[:], by_rows[m][:])
             nc.sync.dma_start(out_rows[:, m, 0:CHUNK], result[:])
-        result = keep.tile([P, ROW_TILES, PIECE], F32, name="result2")
+        result = keep.tile([P, ROW_TILES, PIECE], F32, name="result2", align_bytes=BURST)
         nc.vector.tensor_copy(result[:], paired[:])
         nc.sync.dma_start(out_rows[:, :, CHUNK : V - PIECE], result[:])
-        result = keep.tile([P, ROW_TILES, PIECE], F32, name="result%d" % last)
+        result = keep.tile([P, ROW_TILES, PIECE], F32, name="result%d" % last, align_bytes=BURST)
         nc.vector.tensor_copy(result[:, 0, :], apart[0])
         nc.sync.dma_start(out_rows[:, 0, V - PIECE : V], result[:, 0, :])
         nc.scalar.copy(result[:, 1, :], apart[1])

from contextlib import ExitStack

import concourse.mybir as mybir

K, T, S, H, N, V = 1024, 2048, 1024, 512, 256, 512
FLOPS = 2 * K * H * S + 2 * H * N * V

F32 = mybir.dt.float32
BF16 = mybir.dt.bfloat16
I32 = mybir.dt.int32
U32 = mybir.dt.uint32
U16 = mybir.dt.uint16
U8 = mybir.dt.uint8
FP8X4 = mybir.dt.float8_e4m3fn_x4
GELU = mybir.ActivationFunctionType.Gelu_apprx_tanh
MAX = mybir.AluOpType.max

P = 128
PACK = 4
LINE = 4
PASSES = K // (P * PACK)
LIST_ROWS = 16
CHUNK = 256
CHUNKS = V // CHUNK
PIECE = 128
SHORT = PIECE // 2
HALF = H // 2
GROUPS = HALF // (PACK * LINE)
ROW_TILES = N // P
BURST = 256
QUADRANT = 32
QUADRANT_ORDER = (0, 2, 1, 3)
WARM_UPS = (512, 128)
LATE_WARM_UP = 256
EARLY_BANKS = CHUNKS * PACK - 1


def tile_picked_phpool_gelu_p_kernel(tc, x_words, x_scales, w1, w2, offs, out):
    nc = tc.nc
    with ExitStack() as ctx:
        keep = ctx.enter_context(tc.tile_pool(name="keep", bufs=1))
        psum = ctx.enter_context(tc.psum_pool(name="psum", bufs=1))

        w1_rows = [w1[P * PACK * z : P * PACK * (z + 1), :].rearrange("(p j) c -> p j c", j=PACK) for z in range(PASSES)]
        x_rows = [x_words[z].rearrange("p n j -> p (n j)").bitcast(I32) for z in range(PASSES)]
        word_table = [keep.tile([P, T], I32, name="word_table%d" % z, align_bytes=BURST) for z in range(PASSES)]
        w1_pairs = [keep.tile([P, 2, H], F32, name="w1_pair%d" % h, align_bytes=BURST) for h in range(2)]

        nc.sync.dma_start(w1_pairs[0][:], w1_rows[0][:, 0:2])
        offsets = keep.tile([P, S // LIST_ROWS], U16, name="offsets")
        nc.sync.dma_start(offsets[:], offs)
        scale_table = keep.tile([P, T], U8, name="scale_table", tag="scale_table", align_bytes=BURST)
        nc.vector.memset(scale_table[:].bitcast(I32), 0)
        nc.sync.dma_start(scale_table[0:P:4, :].bitcast(I32), x_scales.rearrange("z q c -> q z c").bitcast(I32))
        planes = keep.tile([P, PASSES, S], U8, name="planes", align_bytes=BURST)
        zero = keep.tile([P, 1], F32, name="zero")
        nc.vector.memset(zero[:], 0.0)
        no_bias = keep.tile([P, 1], F32, name="no_bias")
        nc.scalar.activation(no_bias[:], zero[:], GELU)
        nc.vector.memset(planes[:].rearrange("p z s -> p (z s)").bitcast(I32), 0)

        nc.sync.dma_start(word_table[0][:], x_rows[0])
        nc.sync.dma_start(w1_pairs[1][:], w1_rows[0][:, 2:4])
        nc.sync.dma_start(word_table[1][:], x_rows[1])

        def gather(picked, table):
            for first, count, at in ((CHUNK, 2 * CHUNK, CHUNK), (0, CHUNK, 3 * CHUNK), (3 * CHUNK, CHUNK, 0)):
                entries = offsets[:, first // LIST_ROWS : (first + count) // LIST_ROWS]
                nc.vector.tensor_copy(picked[:, at : at + count], table.indirect(entries))

        picked_scales = keep.tile([P, S], U8, name="picked_scales", align_bytes=BURST)
        gather(picked_scales, scale_table[:])

        def move_scales(z):
            for q in QUADRANT_ORDER:
                first = QUADRANT * q + 4 * z
                nc.sync.dma_start(
                    planes[first : first + 4, z].bitcast(I32), picked_scales[first : QUADRANT * (q + 1) : 8, :].bitcast(I32)
                )

        move_scales(0)
        late = keep.tile([P, 3, PACK, HALF], F32, name="late", tag="scale_table", align_bytes=BURST)
        w1_halves = [late[:, h] for h in range(2)]
        for h in range(2):
            nc.sync.dma_start(w1_halves[h], w1_rows[1][:, :, HALF * h : HALF * (h + 1)])
        move_scales(1)
        w2_raw = late[:, 2]
        w2_rows = w2.rearrange("(g t u) n -> t g u n", t=PACK, u=LINE)
        for t in range(PACK):
            nc.sync.dma_start(w2_raw[:, t, :], w2_rows[t])

        w1_codes = [keep.tile([P, H], U32, name="w1_codes%d" % z, align_bytes=64) for z in range(PASSES)]
        w1_scales = [keep.tile([P, H], U8, name="w1_scales%d" % z, align_bytes=64) for z in range(PASSES)]
        w1_grouped = [
            keep.tile([P, PACK * H], BF16, name="w1_grouped%d" % z, tag="grouped%d" % z, align_bytes=64) for z in range(PASSES)
        ]

        dealt = [grouped[:].rearrange("p (t g u j) -> p g t j u", t=PACK, u=LINE, j=PACK) for grouped in w1_grouped]

        def deal_pair(h, t0, t1):
            nc.scalar.copy(
                dealt[0][:, :, t0:t1, 2 * h : 2 * h + 2],
                w1_pairs[h][:].rearrange("p j (g t u) -> p g t j u", t=PACK, u=LINE)[:, :, t0:t1],
            )

        def deal_half(h, t0, t1):
            nc.scalar.copy(
                dealt[1][:, GROUPS * h : GROUPS * (h + 1), t0:t1],
                w1_halves[h].rearrange("p j (g t u) -> p g t j u", t=PACK, u=LINE)[:, :, t0:t1],
            )

        def quantize_w1(z, t0, t1):
            nc.vector.quantize_mx(
                out=w1_codes[z][:, P * t0 : P * t1].bitcast(FP8X4),
                scales=w1_scales[z][:, P * t0 : P * t1],
                in_=w1_grouped[z][:, H * t0 : H * t1],
            )

        scratch_banks = [psum.tile([P, 2 * CHUNK], F32, name="scratch%d" % i, tag="bank%d" % i) for i in range(len(WARM_UPS))]
        banks = [
            [psum.tile([P, 2 * CHUNK], F32, name="y%d%d" % (c, t), tag="bank%d" % (PACK * c + t)) for t in range(PACK)]
            for c in range(CHUNKS)
        ]

        def one_pass(z, c, t, start):
            cols = slice(2 * CHUNK * (CHUNKS - 1 - c), 2 * CHUNK * (CHUNKS - c))
            nc.tensor.matmul_mx(
                out=banks[c][t][:],
                lhsT=w1_codes[z][:, P * t : P * (t + 1)].bitcast(FP8X4),
                lhsT_scale=w1_scales[z][:, P * t : P * (t + 1)],
                rhs=picked_words[z][:, cols].bitcast(FP8X4),
                rhs_scale=planes[4 * z :, z, cols],
                start=start,
                stop=not start,
            )

        all_banks = [(c, t) for c in range(CHUNKS) for t in range(PACK)]
        early_banks, late_banks = all_banks[:EARLY_BANKS], all_banks[EARLY_BANKS:]

        first_words = keep.tile([P, S], U32, name="first_words", align_bytes=64)
        gather(first_words, word_table[0][:].bitcast(U32))

        def warm_up(scratch, width):
            nc.tensor.matmul_mx(
                out=scratch[:, :width],
                lhsT=first_words[:, 3 * CHUNK : 3 * CHUNK + P].bitcast(FP8X4),
                lhsT_scale=picked_scales[:, 3 * CHUNK : 3 * CHUNK + P],
                rhs=first_words[:, CHUNK : CHUNK + width].bitcast(FP8X4),
                rhs_scale=picked_scales[:, CHUNK : CHUNK + width],
                start=True,
                stop=True,
            )

        for scratch, width in zip(scratch_banks, WARM_UPS):
            warm_up(scratch, width)
        deal_pair(0, 0, PACK)
        for t in range(0, PACK, 2):
            deal_pair(1, t, t + 2)
            quantize_w1(0, t, t + 2)
        picked_words = [first_words]
        for c, t in early_banks:
            one_pass(0, c, t, True)
        last_words = keep.tile([P, S], U32, name="last_words", tag="grouped0", align_bytes=64)
        gather(last_words, word_table[1][:].bitcast(U32))

        deal_half(0, 0, PACK)
        for t in range(PACK):
            deal_half(1, t, t + 1)
            quantize_w1(1, t, t + 1)
        picked_words.append(last_words)
        for c, t in early_banks:
            one_pass(1, c, t, False)
        for c, t in late_banks:
            one_pass(1, c, t, True)
            one_pass(0, c, t, False)

        w2_grouped = keep.tile([P, PACK * N], BF16, name="w2_grouped", tag="grouped1", align_bytes=64)
        for m in range(ROW_TILES):
            nc.gpsimd.tensor_scalar(
                w2_grouped[:].rearrange("p (n t) -> p n t", t=PACK)[:, P * m : P * (m + 1)],
                w2_raw.rearrange("p t n -> p n t")[:, P * m : P * (m + 1)],
                1.0,
                0.0,
                mybir.AluOpType.mult,
                mybir.AluOpType.add,
            )

        largers = [keep.tile([P, CHUNK // LINE, PACK, LINE], F32, name="larger%d" % c, tag="larger%d" % c, align_bytes=64) for c in range(CHUNKS)]

        def larger_shared(c, t):
            reads = banks[c][t][:].rearrange("p (r v) -> p r v", r=2)
            one_read = keep.tile([P, CHUNK], F32, name="one_read%d%d" % (c, t), tag="one_read%d%d" % (c, t), align_bytes=64)
            nc.scalar.copy(one_read[:], reads[:, 0, :])
            nc.vector.tensor_tensor(
                largers[c][:, :, t],
                one_read[:].rearrange("p (l u) -> p l u", u=LINE),
                reads[:, 1, :].rearrange("p (l u) -> p l u", u=LINE),
                MAX,
            )

        def larger_on_vector(c, t, v0):
            lines = slice(v0 // LINE, (v0 + PIECE) // LINE)
            reads = banks[c][t][:].rearrange("p (r l u) -> p l u r", r=2, u=LINE)[:, lines]
            nc.vector.tensor_reduce(largers[c][:, lines, t], reads, mybir.AxisListType.X, MAX)

        pieces = [(0, 0, PIECE), (0, PIECE, PIECE), (1, 0, PIECE), (1, PIECE, SHORT), (1, PIECE + SHORT, SHORT)]
        z_grouped = [keep.tile([P, PACK * n], BF16, name="z_grouped%d" % i, align_bytes=64) for i, (c, v0, n) in enumerate(pieces)]

        def gelu(i):
            c, v0, n = pieces[i]
            nc.scalar.activation(
                z_grouped[i][:].rearrange("p (l u t) -> p l t u", u=LINE, t=PACK),
                largers[c][:, v0 // LINE : (v0 + n) // LINE],
                GELU,
                bias=no_bias[:],
            )

        z_codes = [keep.tile([P, n], U32, name="z_codes%d" % i, align_bytes=64) for i, (c, v0, n) in enumerate(pieces)]
        z_scales = [keep.tile([P, n], U8, name="z_scales%d" % i, align_bytes=64) for i, (c, v0, n) in enumerate(pieces)]
        w2_codes, w2_scales = {}, {}

        def quantize_w2(m, behind):
            w2_codes[m] = keep.tile([P, P], U32, name="w2_codes%d" % m, tag=behind, align_bytes=64)
            w2_scales[m] = keep.tile([P, P], U8, name="w2_scales%d" % m, align_bytes=64)
            nc.vector.quantize_mx(
                out=w2_codes[m][:].bitcast(FP8X4), scales=w2_scales[m][:], in_=w2_grouped[:, PACK * P * m : PACK * P * (m + 1)]
            )

        def quantize_z(i):
            nc.vector.quantize_mx(out=z_codes[i][:].bitcast(FP8X4), scales=z_scales[i][:], in_=z_grouped[i][:])

        def product(i, m, acc):
            nc.tensor.matmul_mx(
                out=acc,
                lhsT=w2_codes[m][:].bitcast(FP8X4),
                lhsT_scale=w2_scales[m][:],
                rhs=z_codes[i][:].bitcast(FP8X4),
                rhs_scale=z_scales[i][:],
                start=True,
                stop=True,
            )

        for t in range(PACK):
            larger_shared(0, t)
        larger_shared(1, 0)
        larger_shared(1, 1)
        larger_shared(1, 2)
        warm_up(psum.tile([P, LATE_WARM_UP], F32, name="late_scratch", tag="bank6"), LATE_WARM_UP)
        for v0 in range(0, CHUNK, PIECE):
            larger_on_vector(1, 3, v0)
        gelu(0)
        last = len(pieces) - 1
        by_rows = [psum.tile([P, CHUNK], F32, name="rows%d" % m, tag="bank%d" % m) for m in range(ROW_TILES)]
        paired = psum.tile([P, ROW_TILES, PIECE], F32, name="paired", tag="bank2")
        apart = [psum.tile([P, PIECE], F32, name="apart%d" % m, tag="bank%d" % (3 + m))[:] for m in range(ROW_TILES)]
        gelu(1)
        quantize_w2(0, "one_read12")
        quantize_z(0)
        product(0, 0, by_rows[0][:, 0:PIECE])
        quantize_z(1)
        product(1, 0, by_rows[0][:, PIECE:CHUNK])
        quantize_w2(1, "larger0")
        product(0, 1, by_rows[1][:, 0:PIECE])
        product(1, 1, by_rows[1][:, PIECE:CHUNK])
        for i in range(2, last + 1):
            gelu(i)
            quantize_z(i)
            c, v0, n = pieces[i]
            for m in range(ROW_TILES):
                product(i, m, paired[:, m, :] if n == PIECE else apart[m][:, v0 - PIECE : v0 - PIECE + n])

        out_rows = out.rearrange("(m p) v -> p m v", p=P)
        for m in range(ROW_TILES):
            result = keep.tile([P, CHUNK], F32, name="result%d" % m, align_bytes=BURST)
            nc.scalar.copy(result[:], by_rows[m][:])
            nc.sync.dma_start(out_rows[:, m, 0:CHUNK], result[:])
        result = keep.tile([P, ROW_TILES, PIECE], F32, name="result2", align_bytes=BURST)
        nc.vector.tensor_copy(result[:], paired[:])
        nc.sync.dma_start(out_rows[:, :, CHUNK : V - PIECE], result[:])
        result = keep.tile([P, ROW_TILES, PIECE], F32, name="result%d" % last, align_bytes=BURST)
        nc.vector.tensor_copy(result[:, 0, :], apart[0])
        nc.sync.dma_start(out_rows[:, 0, V - PIECE : V], result[:, 0, :])
        nc.scalar.copy(result[:, 1, :], apart[1])
        nc.scalar.dma_start(out_rows[:, 1, V - PIECE : V], result[:, 1, :])
